import numpy as np, ml_dtypes
CORES = [16,17,18,19,32,33,34,35]
N = 8
import mx_ref
BF = ml_dtypes.bfloat16
def f(rng, *shape):
    return mx_ref.flush((rng.standard_normal(shape, dtype=np.float32) * np.exp2(rng.integers(-2, 3, shape[:-1] + (1,)))).astype(BF))
def wide(rng, *shape, cols=0):
    v = rng.standard_normal(shape, dtype=np.float32) * np.exp2(rng.integers(-12, 13, shape)).astype(np.float32)
    if cols: v *= np.repeat(np.exp2(rng.integers(-cols, cols + 1, shape[:-2] + (1, shape[-1] // 4))) * (rng.random(shape[:-2] + (1, shape[-1] // 4)) > 0.0625), 4, axis=-1).astype(np.float32)
    return mx_ref.flush(v.astype(BF))
def cols(t, e):
    v = np.concatenate([t.reshape(128, -1, 4), np.zeros((128, 1, 4), BF)], axis=1)
    return np.ascontiguousarray(v[:, e]).reshape(128, -1)
def tile(rs):
    return np.stack(rs, axis=2).reshape(128, -1).astype(BF)
def cut(t, i, w=512):
    return t[:, w * i:w * i + w]
def decode(q):
    o = []
    for b in range(4):
        e = np.zeros((128, 128, 4), np.float32); e[np.arange(128), np.arange(128), b] = 1
        o.append(mx_ref.matmul(mx_ref.quantize(e.reshape(128, 512).astype(BF)), q))
    return np.stack(o, axis=2).reshape(128, -1)
T, CK = 256, 48
def gates(g):
    t = np.zeros((128, 512), BF); t[:, :4 * N] = g
    return np.stack([t] * N)
def plus(g):
    return np.maximum(np.abs(g.astype(np.float32)), np.float32(0.0625)).astype(BF)
def apart(rng):
    g = np.zeros((128, 4 * N), BF)
    for e in range(N): g[8 * e:8 * e + 8, 4 * e:4 * e + 4] = plus(f(rng, 8, 4))
    return g
def setup_inputs(rng):
    return {"x": f(rng, N, 128, 4 * T), "wg": gates(f(rng, 128, 4 * N)), "w1": f(rng, N, 128, 2048)}
def setup_inputs_alike(rng):
    d = setup_inputs(rng); d["wg"] = gates(np.tile(f(rng, 128, 4), (1, N))); return d
def setup_inputs_ties(rng):
    d = setup_inputs(rng); d["wg"] = gates(plus(f(rng, 128, 4 * N))); d["x"] = -plus(d["x"])
    for s in range(N):
        k = rng.permutation(np.arange(T) // 5 if s % 2 else np.arange(T) % (T // (CK + 1)))
        d["x"][s] = d["x"][s].reshape(128, T, 4)[:, k].reshape(128, -1)
    return d
def setup_inputs_split(rng):
    d = setup_inputs(rng); g = apart(rng)
    v = d["x"].astype(np.float32).reshape(N, 128, T, 4)
    for s in range(N):
        p = rng.permutation(T)
        for e in range(N):
            sign = np.full((1, T, 1), -1, np.float32); sign[:, p[(e * CK + np.arange(CK)) % T]] = 1
            v[s, 8 * e:8 * e + 8] = np.abs(v[s, 8 * e:8 * e + 8]) * sign
    d["x"] = v.reshape(N, 128, 4 * T).astype(BF); d["wg"] = gates(g); return d
def setup_inputs_zeros(rng):
    d = setup_inputs(rng); g = apart(rng)
    v = d["x"].astype(np.float32).reshape(N, 128, T, 4)
    for s in range(N):
        for e in range(N):
            p = rng.permutation(T); u = np.abs(v[s, 8 * e:8 * e + 8])
            u[:, p[CK // 2:CK // 2 + CK]] = np.where(rng.random((8, CK, 4)) < 0.5, np.float32(-0.0), np.float32(0.0))
            u[:, p[CK // 2 + CK:]] *= np.float32(-1)
            v[s, 8 * e:8 * e + 8] = u
    d["x"] = v.reshape(N, 128, 4 * T).astype(BF); d["wg"] = gates(g); return d
def setup_inputs_spread(rng):
    d = setup_inputs(rng); d["x"] = wide(rng, N, 128, 4 * T, cols=6); return d
def check_inputs(d):
    b = []
    g = d["wg"].astype(np.float32)
    if (g != g[0]).any() or (g[:, :, 4 * N:] != 0).any(): b.append("wg")
    return b
def reference(x, wg, w1):
    took = []
    for s in range(N):
        z = mx_ref.matmul(mx_ref.quantize(wg[s]), mx_ref.quantize(x[s])) + np.float32(0.0)
        took.append([np.argsort(-z[e], kind="stable")[:CK] for e in range(N)])
    y = np.zeros((N, 128, T, 4), np.float32)
    for e in range(N):
        q = mx_ref.quantize(np.concatenate([cols(x[s], took[s][e]) for s in range(N)], axis=1))
        rs = [np.maximum(mx_ref.matmul(mx_ref.quantize(np.ascontiguousarray(cut(w1[e], i))), q), np.float32(0.0)) * np.float32(0.05) for i in range(4)]
        v = decode(mx_ref.quantize(tile(rs))).reshape(128, N, CK, 4)
        for s in range(N): y[s][:, took[s][e]] += v[:, s]
    return {"y": y.reshape(N, 128, 4 * T)}

@@ -1,0 +1,346 @@
+from concourse.bass import DstId, RemoteDMATransfer
+from concourse.mybir import dt, AluOpType as A, ActivationFunctionType as F
+
+CK = 48
+W4 = 4 * CK
+VB = [0, 1, 2, 3]
+SB = [4, 5, 6, 7]
+NV, NS = len(VB), len(SB)
+
+SCRATCH = {}
+
+
+def _sbuf(dtype, names):
+    for w in names.split():
+        n, c = w.split(":")
+        for m in ([n[:-1] + "0", n[:-1] + "1"] if n.endswith("@") else [n]):
+            SCRATCH[m] = ("sbuf", [128, int(c)], dtype)
+
+
+_sbuf("bfloat16", "wgs:32 xs:1024 xp:1024 w1s:2048 ones:516 z:516 d0blk:256 d0cnt:%d hh:1536 gt@:512 cmp@:%d cs@:%d sg@:%d eqb@:256 es@:256 xg@:768"
+      % (256 * NV, 256 * NV, 256 * NV, 256 * NS))
+for _d, _s in (("float8_e4m3fn_x4", "q"), ("uint8", "c")):
+    _sbuf(_d, " ".join("%s%s%s" % (w[0], _s, w[1:]) for w in "x:256 w:512 e:512 t:192 n:528 m:720 g@:128".split()))
+_sbuf("int32", "ic:1 p3:1 h16i:1 q12:1 ib:256 ibm:256")
+_sbuf("float32", "e4:64 p3f:1 h16:1 mk:4 tok0:128 tokv:128 idr:384 pl:640 dg0:160 dg1:160 dg2:160 dg3:160 d01:160 d23:160 dd:160")
+_sbuf("float32", "ds@:768 pb:%d yt:1024 tt@:256 ac@:8 a2@:4 a3@:4 rk@:8 wn@:256 la@:12 lb@:12 ob@:12" % (16 + 8 * W4))
+_sbuf("uint16", "go:64 op:160 ru@:8 ol@:16 of@:12")
+for _b in range(8):
+    SCRATCH["ps%d" % _b] = ("psum", [128, 512], "float32")
+
+SEMAPHORES = ["v", "t", "s", "p", "dwg", "dx", "dw", "lo0", "lo1", "af", "an", "rf", "rn", "ls", "dy"]
+
+
+def rank_program(g, core, T, topo):
+    rank = T.rank_of(core)
+    if rank is None:
+        return
+    N = len(T.cores)
+    near_of = lambda r: [k for k in range(N) if k != r and topo.chip(T.cores[k]) == topo.chip(T.cores[r])]
+    far_of = lambda r: [k for k in range(N) if topo.chip(T.cores[k]) != topo.chip(T.cores[r])]
+    others, far = near_of(rank), far_of(rank)
+    kind = ["far", "near"] if 0 in far else ["near", "far"]
+    X = [{"far": far, "near": others + [rank]}[k] for k in kind]
+    where = {e: (h, a) for h in range(2) for a, e in enumerate(X[h])}
+    far_e = topo.engines(core, T.cores[far[0]])
+    near_e = [e for e in topo.engines(core, T.cores[others[0]]) if e not in far_e]
+
+    Q = {"v": g.vector, "t": g.tensor, "s": g.scalar, "p": g, "y": g.sync}
+    cnt = {"v": 0, "t": 0, "s": 0, "p": 0}
+    seen = {}
+
+    def need(q, *toks):
+        for s, n in toks:
+            if seen.get((q, s), 0) < n:
+                Q[q].wait_ge(T.sem[s], n)
+                seen[(q, s)] = n
+
+    def done(q, ins):
+        ins.then_inc(T.sem[q], 1)
+        cnt[q] += 1
+        return (q, cnt[q])
+
+    V, S, PE = g.vector, g.scalar, g.tensor
+    v = lambda ins: done("v", ins)
+    s = lambda ins: done("s", ins)
+    t = lambda ins: done("t", ins)
+    p = lambda ins: done("p", ins)
+    ts = lambda out, in0, s1, s2, *ops: v(V.tensor_scalar(out, in0, s1, s2, *ops))
+    tt = lambda out, a, b, op: v(V.tensor_tensor(out, a, b, op))
+
+    g.sync.dma_start(T.wgs[:], T.wg[:, 0:32]).then_inc(T.sem.dwg, 16)
+    g.scalar.dma_start(T.xs[:, 512:1024], T.x[:, 512:1024]).then_inc(T.sem.dx, 16)
+    g.sync.dma_start(T.xs[:, 0:512], T.x[:, 0:512]).then_inc(T.sem.dx, 16)
+    g.sync.dma_start(T.w1s[:], T.w1[:]).then_inc(T.sem.dw, 16)
+    DWG, DX, DW = ("dwg", 16), ("dx", 32), ("dw", 16)
+
+    imp = dict(allow_small_or_imprecise_dtypes=True)
+    p_ic = p(g.iota(T.ic[:], [[0, 1]], 0, 1))
+    for k, e in enumerate(X[0] + X[1]):
+        p_e4 = p(g.iota(T.e4[:, 8 * k:8 * k + 8], [[0, 8]], 4 * e, 0, **imp))
+    p_tok = p(g.iota(T.tok0[:], [[32, 8], [1, 16]], 0, 0, **imp))
+    p_ib = p(g.iota(T.ib[:], [[1, 256]], 128, -1))
+    v_ones = v(V.memset(T.ones[:], 1.0))
+    need("p", v_ones)
+    p_z = p(g.affine_select(T.z[:], T.ones[:], [[-1, 516]], A.is_equal, 0.0, 3, 4))
+    p_id = p(g.iota(T.idr[:], [[W4, N], [4, CK]], 16, 0, **imp))
+
+    need("v", p_ic)
+    v_p3 = ts(T.p3[:], T.ic[:], 3, None, A.bitwise_and)
+    v_h16i = ts(T.h16i[:], T.ic[:], 16, None, A.bitwise_and)
+    v_q12 = ts(T.q12[:], T.ic[:], 12, None, A.bitwise_and)
+    need("v", v_p3)
+    v_p3f = ts(T.p3f[:], T.p3[:], 1.0, None, A.mult)
+    need("v", v_h16i)
+    v_h16 = ts(T.h16[:], T.h16i[:], 1.0, None, A.mult)
+    need("v", v_p3f, p_e4)
+    v_go = ts(T.go[:], T.e4[:], T.p3f[:, 0:1], None, A.add)
+    v_d1 = v(V.memset(T.d0cnt[:], 1.0))
+    need("v", DWG, v_go)
+    v_gt = v(V.tensor_copy(T.gt0[:, 0:256], T.wgs[:, 0:32].indirect(T.go[:, 0:16])))
+    need("s", DWG, v_go)
+    s_gt0 = s(S.activation(T.gt0[:, 256:512], T.wgs[:, 0:32].indirect(T.go[:, 16:32]), F.Copy))
+    s_gt1 = s(S.activation(T.gt1[:], T.wgs[:, 0:32].indirect(T.go[:, 32:64]), F.Copy))
+    need("v", v_gt, s_gt0)
+    v_gq = [v(V.quantize_mx(T.gq0[:, 0:128], T.gc0[:, 0:128], T.gt0[:, 0:512])), None]
+
+    need("v", DX)
+    v_xq = v(V.quantize_mx(T.xq[:, 0:256], T.xc[:, 0:256], T.xs[:, 0:1024]))
+    v_z = [v(V.memset(T["ac%d" % h][:, 7:8], 0.0)) for h in range(2)]
+    plane = lambda k: (T.xp[:, 256 * k:256 * k + 256], T.xs[:, k:1024:4])
+    v_xp = v(V.tensor_copy(*plane(3)))
+    need("s", DX)
+    s(S.activation(*plane(0), F.Copy))
+    sv, ss = [T.ps4, T.ps6], [T.ps5, T.ps7]
+    t_sv, t_ss = [None, None], [None, None]
+
+    def score(h):
+        need("t", v_xq, v_gq[h])
+        mm = lambda out: t(PE.matmul_mx(out, T["gq%d" % h][:, 0:128], T["gc%d" % h][:, 0:128], T.xq[:, 0:256], T.xc[:, 0:256], True, True))
+        t_sv[h] = mm(sv[h][:, 0:256])
+        t_ss[h] = mm(ss[h][:, 0:256])
+
+    s_cnt, v_cnt, v_es, v_svread = [None, None], [None, None], [None, None], [None, None]
+    const = {}
+
+    def count(h):
+        P, own, cm, PS, sg, ac = sv[h], T["tt%d" % h], T["cmp%d" % h], ss[h], T["sg%d" % h], T["ac%d" % h]
+        need("v", t_sv[h])
+        v_tt = v(V.transpose(own[:], P[:, 0:256]))
+        need("s", t_ss[h], v_tt, v_z[h])
+        sgn = [s(S.activation(sg[:, 256 * u:256 * u + 256], PS[:, 0:256], F.Sign, bias=own[:, 32 * b:32 * b + 1], scale=-1.0)) for u, b in enumerate(SB)]
+        for u, b in enumerate(SB):
+            need("s", sgn[u])
+            m = 256 * u + 32 * (b + 1)
+            lo = sg[:, 256 * u:m]
+            s_cnt[h] = s(S.activation(lo, lo, F.Sign, bias=1.0, scale=-2.0, accum_out=ac[:, u:u + 1]))
+            if b < 7:
+                hi = sg[:, m:256 * u + 256]
+                s_cnt[h] = s(S.activation(hi, hi, F.Sign, bias=-1.0, scale=-2.0, accum_out=ac[:, NS + u:NS + u + 1]))
+        need("v", v_tt)
+        v_eq = tt(T["eqb%d" % h][:], P[:, 0:256], own[:], A.is_equal)
+        for u, b in enumerate(VB):
+            m = 32 * (b + 1)
+            ts(cm[:, 256 * u:256 * u + m], P[:, 0:m], own[:, 32 * b:32 * b + 1], None, A.is_ge)
+            v_svread[h] = ts(cm[:, 256 * u + m:256 * u + 256], P[:, m:256], own[:, 32 * b:32 * b + 1], None, A.is_gt)
+        if h == 0:
+            need("v", v_d1, p_ib)
+            v_ibm = ts(T.ibm[:], T.ib[:], 31, None, A.bitwise_and)
+            const["d0"] = v(V.memset(T.d0cnt[:, 0:256 * NV:256], 0.0))
+            need("v", v_ibm)
+            const["blk"] = ts(T.d0blk[:], T.ibm[:], 0, None, A.not_equal)
+            need("v", s_gt1)
+            v_gq[1] = v(V.quantize_mx(T.gq1[:, 0:128], T.gc1[:, 0:128], T.gt1[:, 0:512]))
+        need("v", v_svread[h], const["d0"])
+        v_cnt[h] = v(V.tensor_tensor_scan(T["cs%d" % h][:], T.d0cnt[:], cm[:], 0.0, A.mult, A.add))
+        need("v", v_eq, const["blk"])
+        v_es[h] = v(V.tensor_tensor_scan(T["es%d" % h][:], T.d0blk[:], T["eqb%d" % h][:], 0.0, A.mult, A.add))
+        if h == 0:
+            need("v", p_tok, v_h16)
+            const["tok"] = ts(T.tokv[:], T.tok0[:], T.h16[:, 0:1], None, A.add)
+            const["wn"] = [v(V.memset(T["wn%d" % k][:, 0:CK], 0.0)) for k in range(2)]
+
+    def invert(h, queues):
+        B = lambda n: T["%s%d" % (n, h)]
+        need("v", v_cnt[h], v_es[h])
+        tt(B("rk")[:, 0:NV], B("cs")[:, 255:256 * NV:256], B("es")[:, 31:32 * NV:32], A.subtract)
+        need("v", s_cnt[h])
+        x2 = tt(B("a2")[:, 0:NS], B("ac")[:, 0:NS], B("ac")[:, NS:2 * NS], A.add)
+        need("v", x2)
+        x3 = ts(B("a3")[:, 0:NS], B("a2")[:, 0:NS], 0.5, 128.0, A.mult, A.add)
+        need("v", x3)
+        r2 = tt(B("rk")[:, NV:8], B("a3")[:, 0:NS], B("es")[:, 32 * NV + 31:256:32], A.subtract)
+        need("v", r2)
+        ru = ts(B("ru")[:, 0:8], B("rk")[:, 0:8], 1.0, None, A.mult)
+        need("v", ru, const["tok"], const["wn"][h])
+        w = v(V.tensor_copy(B("wn")[:, 0:256].indirect(B("ru")[:, 0:8]), T.tokv[:, 0:128]))
+        for k in range(8):
+            a, half, q = k // 2, k % 2, queues[k % len(queues)]
+            need(q, w)
+            lst = B("wn")[32 * a + 16 * half:32 * a + 16 * half + 8, 0:CK]
+            Q[q].dma_start(B("lb" if half else "la")[:, 3 * a:3 * a + 3], lst).then_inc(T.sem["lo%d" % h], 16)
+
+    v_of, v_ob = [None, None], [None, None]
+
+    def pick(h, qbuf, cbuf):
+        xg, of = T["xg%d" % h], T["of%d" % h]
+        need("v", ("lo%d" % h, 128))
+        v_ob[h] = tt(T["ob%d" % h][:], T["la%d" % h][:], T["lb%d" % h][:], A.add)
+        need("v", v_ob[h])
+        v_of[h] = ts(of[:], T["ob%d" % h][:], 1.0, None, A.mult)
+        gat = lambda k: (xg[:, k:4 * W4:4], T.xp[:, 256 * k:256 * k + 256].indirect(of[:, 0:12]))
+        need("s", s_xp, v_xp, v_of[h])
+        need("v", s_xp, v_xp, v_of[h])
+        for k in (0, 1):
+            s_g = s(S.activation(*gat(k), F.Copy))
+        for k in (2, 3):
+            v_g = v(V.tensor_copy(*gat(k)))
+        need("v", s_g, v_g)
+        return v(V.quantize_mx(qbuf, cbuf, xg[:, 0:4 * W4]))
+
+    ls = [0]
+
+    def send(parts):
+        for z in ("q", "c"):
+            tr = []
+            for d, src, a, dst, b, sem in parts:
+                rid, pid, _ = topo.addr(T.cores[d])
+                k, eng = (far.index(d), far_e) if d in far else (others.index(d), near_e)
+                sa, da = T[src + z][:, a:a + CK], T[dst + z][:, b:b + CK]
+                if z == "q":
+                    sa, da = sa.bitcast(dt.uint8), da.bitcast(dt.uint8)
+                tr.append(RemoteDMATransfer(dst_ids=[DstId(rid=rid, pnc=pid)], dma_engine_mask=(1 << eng[2 * k]) | (1 << eng[2 * k + 1]),
+                                            remote_sem=T.sem[sem], src=sa, dst=da))
+                ls[0] += 2
+            g.remote_dma_fused(tr, local_sem=T.sem.ls)
+
+    in_far = lambda d: CK * far_of(d).index(rank)
+    in_near = lambda d: CK * near_of(d).index(rank)
+
+    def dispatch(h):
+        src = "t" if kind[h] == "far" else "n"
+        x = pick(h, T[src + "q"][:, 0:W4], T[src + "c"][:, 0:W4])
+        need("p", x)
+        if kind[h] == "far":
+            send([(d, "t", CK * k, "n", 336 + in_far(d), "af") for k, d in enumerate(far)])
+        else:
+            send([(d, "n", CK * k, "n", W4 + in_near(d), "an") for k, d in enumerate(others)])
+        return x
+
+    table = T.pl[:, 384:640]
+    v_chain = [None, None]
+
+    def chain(h):
+        need("v", v_ob[h])
+        for m in range(3):
+            x = ts(T["ol%d" % h][:, m:16:4], T["ob%d" % h][:, m:12:3], 1.0, None, A.mult)
+        need("v", x, v_fresh, p_id)
+        for e in sorted(X[h]):
+            a = where[e][1]
+            at = table.indirect(T["ol%d" % h][:, 4 * a:4 * a + 3])
+            o = W4 * h + CK * a
+            if e == 0:
+                x = v(V.memset(T.pl[:, o:o + CK], 0.0))
+            else:
+                x = v(V.tensor_copy(T.pl[:, o:o + CK], at))
+            need("v", x)
+            x = v(V.tensor_copy(at, T.idr[:, CK * e:CK * e + CK]))
+            need("v", x)
+        v_chain[h] = x
+
+    score(0)
+    count(0)
+    score(1)
+    for k in (1, 2):
+        s_xp = s(S.activation(*plane(k), F.Copy))
+    invert(0, ["y"])
+    count(1)
+    invert(1, ["y", "s"])
+    v_x = [dispatch(0), None]
+    need("v", DW)
+    v_wq = v(V.quantize_mx(T.wq[:, 0:512], T.wc[:, 0:512], T.w1s[:, 0:2048]))
+    v_fresh = v(V.memset(table, 0.0))
+    v_x[1] = dispatch(1)
+    chain(0)
+    chain(1)
+    need("v", p_z)
+    for b in range(4):
+        v_ebq = v(V.quantize_mx(T.eq[:, 128 * b:128 * b + 128], T.ec[:, 128 * b:128 * b + 128], T.z[:, 3 - b:515 - b]))
+
+    def addresses():
+        need("v", v_q12)
+        for k in range(4):
+            v_mk = ts(T.mk[:, k:k + 1], T.q12[:], float(4 * k), None, A.is_equal)
+        v(V.memset(T.pb[:, 0:16], 0.0))
+        need("s", v_chain[1], v_mk)
+        dg = [T["dg%d" % k] for k in range(4)]
+        for k in range(4):
+            s_dg = s(S.activation(dg[k][:], T.pl[:, k:640:4], F.Identity, scale=T.mk[:, k:k + 1]))
+        need("v", s_dg)
+        tt(T.d01[:], dg[0][:], dg[1][:], A.add)
+        need("v", tt(T.d23[:], dg[2][:], dg[3][:], A.add))
+        need("v", tt(T.dd[:], T.d01[:], T.d23[:], A.add))
+        return ts(T.op[:], T.dd[:], T.p3f[:, 0:1], None, A.add)
+
+    def expert():
+        need("t", v_wq, v_x[kind.index("near")], ("an", 12), ("af", 16))
+        W8 = 2 * W4
+        tm = [t(PE.matmul_mx(T["ps%d" % i][:, 0:W8], T.wq[:, 128 * i:128 * i + 128], T.wc[:, 128 * i:128 * i + 128],
+                             T.nq[:, 144:528], T["nc"][:, 144:528], True, True)) for i in range(4)]
+        for i in (0, 2):
+            need("s", tm[i])
+            s_r = s(S.activation(T.hh[:, i:4 * W8:4], T["ps%d" % i][:, 0:W8], F.Relu, scale=0.05))
+            need("v", tm[i + 1])
+            v_r = ts(T.hh[:, i + 1:4 * W8:4], T["ps%d" % (i + 1)][:, 0:W8], 0.0, 0.05, A.max, A.mult)
+        need("v", s_r, v_r)
+        x = v(V.quantize_mx(T.mq[:, 144:528], T.mc[:, 144:528], T.hh[:, 0:4 * W8]))
+        need("p", x)
+        send([(d, "m", 336 + CK * k, "m", 528 + in_far(d), "rf") for k, d in enumerate(far)]
+             + [(d, "m", W4 + CK * k, "m", in_near(d), "rn") for k, d in enumerate(others)])
+        return x, [s_r, v_r]
+
+    v_h, free = expert()
+    v_op = addresses()
+
+    def unpack(pieces, banks, qv, cv, ready):
+        need("t", v_ebq, *ready)
+        tm = [t(PE.matmul_mx(T["ps%d" % k][:, 0:W4], T.eq[:, 128 * b:128 * b + 128], T.ec[:, 128 * b:128 * b + 128], qv, cv, True, True)) for b, k in enumerate(banks)]
+        for b in (0, 2):
+            for q, f in (("s", b), ("v", b + 1)):
+                need(q, tm[f])
+                for lo, hi, buf, at in pieces:
+                    o, i = buf[:, 4 * at + f:4 * (at + hi - lo):4], T["ps%d" % banks[f]][:, lo:hi]
+                    if q == "s":
+                        s_r = s(S.activation(o, i, F.Copy))
+                    else:
+                        v_r = v(V.tensor_copy(o, i))
+        return [s_r, v_r]
+
+    for c in range(2):
+        ds = T["ds%d" % c]
+        pieces = [(0, W4, ds, 0)]
+        if c == 0:
+            z = CK * where[0][1]
+            pieces = [(z, z + CK, T.pb, 4)] + [(lo, hi, ds, lo) for lo, hi in ((0, z), (z + CK, W4)) if lo < hi]
+        if kind[c] == "far":
+            ready = unpack(pieces, [0, 1, 2, 3], T.mq[:, 528:720], T.mc[:, 528:720], [("rf", 16)] + free)
+        else:
+            ready = unpack(pieces, [4, 5, 6, 7], T.mq[:, 0:W4], T.mc[:, 0:W4], [("rn", 12), v_h, v_svread[1], s_cnt[1]])
+        need("v", v_op, *ready)
+        for e in sorted(X[c]):
+            if e == 0:
+                continue
+            d, o, k = W4 * where[e][1], 16 + W4 * e, 48 * c + 12 * where[e][1]
+            x = tt(T.pb[:, o:o + W4], T.pb[:, 0:o].indirect(T.op[:, k:k + 12]), ds[:, d:d + W4], A.add)
+            need("v", x)
+    win = T.pb[:, 0:16 + N * W4]
+    need("s", x)
+    s_y = s(S.activation(T.yt[:, 512:1024], win.indirect(T.op[:, 128:160]), F.Copy))
+    v_y = v(V.tensor_copy(T.yt[:, 0:512], win.indirect(T.op[:, 96:128])))
+    need("y", v_y)
+    g.sync.dma_start(T.y[:, 0:512], T.yt[:, 0:512]).then_inc(T.sem.dy, 16)
+    need("s", s_y)
+    g.scalar.dma_start(T.y[:, 512:1024], T.yt[:, 512:1024]).then_inc(T.sem.dy, 16)
+
+    need("p", ("ls", ls[0]), ("dwg", 16), DX, DW, ("lo0", 128), ("lo1", 128), ("af", 16), ("an", 12), ("rf", 16), ("rn", 12), ("dy", 32))
+    need("p", *[(q, cnt[q]) for q in ("v", "s", "t", "p")])

@@ -3,9 +3,8 @@ from concourse.mybir import dt, AluOpType as A, ActivationFunctionType as F
 
 CK = 48
 W4 = 4 * CK
-VB = [0, 1, 2, 3]
-SB = [4, 5, 6, 7]
-NV, NS = len(VB), len(SB)
+SB = [[5, 6, 7], [3, 4, 5, 6, 7]]
+SW = 257
 
 SCRATCH = {}
 
@@ -17,18 +16,18 @@ def _sbuf(dtype, names):
             SCRATCH[m] = ("sbuf", [128, int(c)], dtype)
 
 
-_sbuf("bfloat16", "wgs:32 xs:1024 xp:1024 w1s:2048 ones:516 z:516 d0blk:256 d0cnt:%d hh:1536 gt@:512 cmp@:%d cs@:%d sg@:%d eqb@:256 es@:256 xg@:768"
-      % (256 * NV, 256 * NV, 256 * NV, 256 * NS))
+_sbuf("bfloat16", "wgs:32 xs:1024 xp:1024 w1s:2048 ones:516 z:516 col:256 blk:256 tok0:128 tokv:128 hh@:768 gt@:512 cmp@:2048 cs@:1024 sg@:%d "
+      "rk@:8 eqb@:256 es@:256 wn@:256 dp@:96 tw@:96 yl@:12 xg@:768" % (8 * SW))
 for _d, _s in (("float8_e4m3fn_x4", "q"), ("uint8", "c")):
     _sbuf(_d, " ".join("%s%s%s" % (w[0], _s, w[1:]) for w in "x:256 w:512 e:512 t:192 n:528 m:720 g@:128".split()))
-_sbuf("int32", "ic:1 p3:1 h16i:1 q12:1 ib:256 ibm:256")
-_sbuf("float32", "e4:64 p3f:1 h16:1 mk:4 tok0:128 tokv:128 idr:384 pl:640 dg0:160 dg1:160 dg2:160 dg3:160 d01:160 d23:160 dd:160")
-_sbuf("float32", "ds@:768 pb:%d yt:1024 tt@:256 ac@:8 a2@:4 a3@:4 rk@:8 wn@:256 la@:12 lb@:12 ob@:12" % (16 + 8 * W4))
-_sbuf("uint16", "go:64 op:160 ru@:8 ol@:16 of@:12")
+_sbuf("int32", "ic:1 pi:5")
+_sbuf("float32", "e4:64 pf:5 do0:6 mk:4 idr:384 pl:640 dg0:160 dg1:160 dg2:160 dg3:160 d01:160 d23:160 dd:160")
+_sbuf("float32", "ds@:768 pb:%d yt:1024 tt@:256 ac@:16" % (16 + 8 * W4))
+_sbuf("uint16", "go:64 do:6 op:160 ru@:8 ol@:16 of@:12")
 for _b in range(8):
     SCRATCH["ps%d" % _b] = ("psum", [128, 512], "float32")
 
-SEMAPHORES = ["v", "t", "s", "p", "dwg", "dx", "dw", "lo0", "lo1", "af", "an", "rf", "rn", "ls", "dy"]
+SEMAPHORES = ["v", "t", "s", "p", "dwg", "dx", "dw", "af", "an", "rf", "rn", "ls", "dy"]
 
 
 def rank_program(g, core, T, topo):
@@ -39,8 +38,7 @@ def rank_program(g, core, T, topo):
     near_of = lambda r: [k for k in range(N) if k != r and topo.chip(T.cores[k]) == topo.chip(T.cores[r])]
     far_of = lambda r: [k for k in range(N) if topo.chip(T.cores[k]) != topo.chip(T.cores[r])]
     others, far = near_of(rank), far_of(rank)
-    kind = ["far", "near"] if 0 in far else ["near", "far"]
-    X = [{"far": far, "near": others + [rank]}[k] for k in kind]
+    X = [far, others + [rank]]
     where = {e: (h, a) for h in range(2) for a, e in enumerate(X[h])}
     far_e = topo.engines(core, T.cores[far[0]])
     near_e = [e for e in topo.engines(core, T.cores[others[0]]) if e not in far_e]
@@ -68,34 +66,37 @@ def rank_program(g, core, T, topo):
     ts = lambda out, in0, s1, s2, *ops: v(V.tensor_scalar(out, in0, s1, s2, *ops))
     tt = lambda out, a, b, op: v(V.tensor_tensor(out, a, b, op))
 
-    g.sync.dma_start(T.wgs[:], T.wg[:, 0:32]).then_inc(T.sem.dwg, 16)
-    g.scalar.dma_start(T.xs[:, 512:1024], T.x[:, 512:1024]).then_inc(T.sem.dx, 16)
-    g.sync.dma_start(T.xs[:, 0:512], T.x[:, 0:512]).then_inc(T.sem.dx, 16)
+    g.scalar.dma_start(T.wgs[:], T.wg[:, 0:32]).then_inc(T.sem.dwg, 16)
+    g.sync.dma_start(T.xs[:], T.x[:]).then_inc(T.sem.dx, 16)
     g.sync.dma_start(T.w1s[:], T.w1[:]).then_inc(T.sem.dw, 16)
-    DWG, DX, DW = ("dwg", 16), ("dx", 32), ("dw", 16)
+    DWG, DX, DW = ("dwg", 16), ("dx", 16), ("dw", 16)
 
     imp = dict(allow_small_or_imprecise_dtypes=True)
     p_ic = p(g.iota(T.ic[:], [[0, 1]], 0, 1))
-    for k, e in enumerate(X[0] + X[1]):
-        p_e4 = p(g.iota(T.e4[:, 8 * k:8 * k + 8], [[0, 8]], 4 * e, 0, **imp))
+    for h in range(2):
+        p_e4 = p(g.iota(T.e4[:, 32 * h:32 * h + 32], [[4, 4], [0, 8]], 4 * min(X[h]), 0, **imp))
     p_tok = p(g.iota(T.tok0[:], [[32, 8], [1, 16]], 0, 0, **imp))
-    p_ib = p(g.iota(T.ib[:], [[1, 256]], 128, -1))
+    p_do = p(g.iota(T.do0[:], [[16, 3], [0, 2]], 0, 0, **imp))
+    p_col = p(g.iota(T.col[:], [[0, 8], [1, 32]], 0, 0, **imp))
+    for h in range(2):
+        p_m = p(g.iota(T["sg%d" % h][:, SW - 1:8 * SW:SW], [[-32, 8]], -32, 0, **imp))
+    p_wn = [p(g.iota(T["wn%d" % h][:, 0:CK], [[0, CK]], 0, 0, **imp)) for h in range(2)]
     v_ones = v(V.memset(T.ones[:], 1.0))
     need("p", v_ones)
     p_z = p(g.affine_select(T.z[:], T.ones[:], [[-1, 516]], A.is_equal, 0.0, 3, 4))
     p_id = p(g.iota(T.idr[:], [[W4, N], [4, CK]], 16, 0, **imp))
 
     need("v", p_ic)
-    v_p3 = ts(T.p3[:], T.ic[:], 3, None, A.bitwise_and)
-    v_h16i = ts(T.h16i[:], T.ic[:], 16, None, A.bitwise_and)
-    v_q12 = ts(T.q12[:], T.ic[:], 12, None, A.bitwise_and)
-    need("v", v_p3)
-    v_p3f = ts(T.p3f[:], T.p3[:], 1.0, None, A.mult)
-    need("v", v_h16i)
-    v_h16 = ts(T.h16[:], T.h16i[:], 1.0, None, A.mult)
-    need("v", v_p3f, p_e4)
-    v_go = ts(T.go[:], T.e4[:], T.p3f[:, 0:1], None, A.add)
-    v_d1 = v(V.memset(T.d0cnt[:], 1.0))
+    for k, m in enumerate((3, 31, 16, 15, 12)):
+        x = ts(T.pi[:, k:k + 1], T.ic[:], m, None, A.bitwise_and)
+    need("v", x)
+    v_pf = v(V.tensor_copy(T.pf[:], T.pi[:]))
+    p3, p31, p16, p15, p12 = [T.pf[:, k:k + 1] for k in range(5)]
+    need("v", v_pf, p_e4)
+    v_go = ts(T.go[:], T.e4[:], p3, None, A.add)
+    need("v", p_tok, p_do)
+    v_tok = ts(T.tokv[:], T.tok0[:], p16, None, A.add)
+    v_do = ts(T.do[:], T.do0[:], p15, None, A.add)
     need("v", DWG, v_go)
     v_gt = v(V.tensor_copy(T.gt0[:, 0:256], T.wgs[:, 0:32].indirect(T.go[:, 0:16])))
     need("s", DWG, v_go)
@@ -103,14 +104,12 @@ def rank_program(g, core, T, topo):
     s_gt1 = s(S.activation(T.gt1[:], T.wgs[:, 0:32].indirect(T.go[:, 32:64]), F.Copy))
     need("v", v_gt, s_gt0)
     v_gq = [v(V.quantize_mx(T.gq0[:, 0:128], T.gc0[:, 0:128], T.gt0[:, 0:512])), None]
+    need("v", p_col)
+    v_blk = ts(T.blk[:], T.col[:], p31, None, A.not_equal)
 
     need("v", DX)
     v_xq = v(V.quantize_mx(T.xq[:, 0:256], T.xc[:, 0:256], T.xs[:, 0:1024]))
-    v_z = [v(V.memset(T["ac%d" % h][:, 7:8], 0.0)) for h in range(2)]
     plane = lambda k: (T.xp[:, 256 * k:256 * k + 256], T.xs[:, k:1024:4])
-    v_xp = v(V.tensor_copy(*plane(3)))
-    need("s", DX)
-    s(S.activation(*plane(0), F.Copy))
     sv, ss = [T.ps4, T.ps6], [T.ps5, T.ps7]
     t_sv, t_ss = [None, None], [None, None]
 
@@ -120,123 +119,158 @@ def rank_program(g, core, T, topo):
         t_sv[h] = mm(sv[h][:, 0:256])
         t_ss[h] = mm(ss[h][:, 0:256])
 
-    s_cnt, v_cnt, v_es, v_svread = [None, None], [None, None], [None, None], [None, None]
-    const = {}
+    v_own, v_es, v_e, v_rk, s_rk, s_sg = [None, None], [None, None], [None, None], [None, None], [None, None], [{}, {}]
+    slot = lambda h, b: T["cs%d" % h][:, 128 * b + 127:128 * b + 128]
 
-    def count(h):
-        P, own, cm, PS, sg, ac = sv[h], T["tt%d" % h], T["cmp%d" % h], ss[h], T["sg%d" % h], T["ac%d" % h]
+    def own(h):
         need("v", t_sv[h])
-        v_tt = v(V.transpose(own[:], P[:, 0:256]))
-        need("s", t_ss[h], v_tt, v_z[h])
-        sgn = [s(S.activation(sg[:, 256 * u:256 * u + 256], PS[:, 0:256], F.Sign, bias=own[:, 32 * b:32 * b + 1], scale=-1.0)) for u, b in enumerate(SB)]
-        for u, b in enumerate(SB):
-            need("s", sgn[u])
-            m = 256 * u + 32 * (b + 1)
-            lo = sg[:, 256 * u:m]
-            s_cnt[h] = s(S.activation(lo, lo, F.Sign, bias=1.0, scale=-2.0, accum_out=ac[:, u:u + 1]))
+        v_own[h] = v(V.transpose(T["tt%d" % h][:], sv[h][:, 0:256]))
+
+    def equal(h):
+        need("v", v_own[h])
+        x = tt(T["eqb%d" % h][:], sv[h][:, 0:256], T["tt%d" % h][:], A.is_equal)
+        need("v", x, v_blk)
+        v_es[h] = v(V.tensor_tensor_scan(T["es%d" % h][:], T.blk[:], T["eqb%d" % h][:], 0.0, A.mult, A.add))
+
+    def compare(h):
+        P, cm = sv[h], T["cmp%d" % h]
+        need("v", v_own[h])
+        for b in range(8 - len(SB[h])):
+            m, o = 32 * (b + 1), T["tt%d" % h][:, 32 * b:32 * b + 1]
+            ts(cm[:, 256 * b:256 * b + m], P[:, 0:m], o, None, A.is_ge)
+            x = ts(cm[:, 256 * b + m:256 * b + 256], P[:, m:256], o, None, A.is_gt)
+        return x
+
+    def total(h, x):
+        cm = T["cmp%d" % h]
+        need("v", x)
+        for b in range(8 - len(SB[h])):
+            v_rk[h] = v(V.tensor_tensor_scan(T["cs%d" % h][:, 128 * b:128 * b + 128], cm[:, 256 * b:256 * b + 128], cm[:, 256 * b + 128:256 * b + 256],
+                                             0.0, A.add, A.add))
+
+    def signs(h, blocks):
+        need("s", t_ss[h], v_own[h])
+        for b in blocks:
+            s_sg[h][b] = s(S.activation(T["sg%d" % h][:, SW * b:SW * b + 256], ss[h][:, 0:256], F.Sign, bias=T["tt%d" % h][:, 32 * b:32 * b + 1], scale=-1.0))
+
+    def sums(h, blocks):
+        sg, ac = T["sg%d" % h], T["ac%d" % h]
+        last = {}
+        for b in blocks:
+            need("s", s_sg[h][b], p_m)
+            m = SW * b + 32 * (b + 1)
+            lo, hi = sg[:, SW * b:m], sg[:, m:SW * b + SW]
+            last[b] = s(S.activation(lo, lo, F.Relu, accum_out=ac[:, b:b + 1]))
             if b < 7:
-                hi = sg[:, m:256 * u + 256]
-                s_cnt[h] = s(S.activation(hi, hi, F.Sign, bias=-1.0, scale=-2.0, accum_out=ac[:, NS + u:NS + u + 1]))
-        need("v", v_tt)
-        v_eq = tt(T["eqb%d" % h][:], P[:, 0:256], own[:], A.is_equal)
-        for u, b in enumerate(VB):
-            m = 32 * (b + 1)
-            ts(cm[:, 256 * u:256 * u + m], P[:, 0:m], own[:, 32 * b:32 * b + 1], None, A.is_ge)
-            v_svread[h] = ts(cm[:, 256 * u + m:256 * u + 256], P[:, m:256], own[:, 32 * b:32 * b + 1], None, A.is_gt)
-        if h == 0:
-            need("v", v_d1, p_ib)
-            v_ibm = ts(T.ibm[:], T.ib[:], 31, None, A.bitwise_and)
-            const["d0"] = v(V.memset(T.d0cnt[:, 0:256 * NV:256], 0.0))
-            need("v", v_ibm)
-            const["blk"] = ts(T.d0blk[:], T.ibm[:], 0, None, A.not_equal)
-            need("v", s_gt1)
-            v_gq[1] = v(V.quantize_mx(T.gq1[:, 0:128], T.gc1[:, 0:128], T.gt1[:, 0:512]))
-        need("v", v_svread[h], const["d0"])
-        v_cnt[h] = v(V.tensor_tensor_scan(T["cs%d" % h][:], T.d0cnt[:], cm[:], 0.0, A.mult, A.add))
-        need("v", v_eq, const["blk"])
-        v_es[h] = v(V.tensor_tensor_scan(T["es%d" % h][:], T.d0blk[:], T["eqb%d" % h][:], 0.0, A.mult, A.add))
-        if h == 0:
-            need("v", p_tok, v_h16)
-            const["tok"] = ts(T.tokv[:], T.tok0[:], T.h16[:, 0:1], None, A.add)
-            const["wn"] = [v(V.memset(T["wn%d" % k][:, 0:CK], 0.0)) for k in range(2)]
+                last[b] = s(S.activation(hi, hi, F.Relu, scale=-1.0, accum_out=ac[:, 8 + b:9 + b]))
+        for b in blocks:
+            need("s", last[b])
+            s_rk[h] = s(S.activation(slot(h, b), ac[:, b:b + 1], F.Identity, scale=-1.0, bias=ac[:, 8 + b:9 + b] if b < 7 else 256.0))
 
-    def invert(h, queues):
+    v_of = [None, None]
+
+    def invert(h):
         B = lambda n: T["%s%d" % (n, h)]
-        need("v", v_cnt[h], v_es[h])
-        tt(B("rk")[:, 0:NV], B("cs")[:, 255:256 * NV:256], B("es")[:, 31:32 * NV:32], A.subtract)
-        need("v", s_cnt[h])
-        x2 = tt(B("a2")[:, 0:NS], B("ac")[:, 0:NS], B("ac")[:, NS:2 * NS], A.add)
-        need("v", x2)
-        x3 = ts(B("a3")[:, 0:NS], B("a2")[:, 0:NS], 0.5, 128.0, A.mult, A.add)
-        need("v", x3)
-        r2 = tt(B("rk")[:, NV:8], B("a3")[:, 0:NS], B("es")[:, 32 * NV + 31:256:32], A.subtract)
-        need("v", r2)
-        ru = ts(B("ru")[:, 0:8], B("rk")[:, 0:8], 1.0, None, A.mult)
-        need("v", ru, const["tok"], const["wn"][h])
-        w = v(V.tensor_copy(B("wn")[:, 0:256].indirect(B("ru")[:, 0:8]), T.tokv[:, 0:128]))
-        for k in range(8):
-            a, half, q = k // 2, k % 2, queues[k % len(queues)]
-            need(q, w)
-            lst = B("wn")[32 * a + 16 * half:32 * a + 16 * half + 8, 0:CK]
-            Q[q].dma_start(B("lb" if half else "la")[:, 3 * a:3 * a + 3], lst).then_inc(T.sem["lo%d" % h], 16)
+        need("v", v_rk[h], s_rk[h], v_es[h])
+        need("v", tt(B("rk")[:], B("cs")[:, 127:1024:128], B("es")[:, 31:256:32], A.subtract))
+        x = v(V.tensor_copy(B("ru")[:], B("rk")[:]))
+        need("v", x, v_tok, p_wn[h])
+        x = v(V.tensor_copy(B("wn")[:, 0:256].indirect(B("ru")[:, 0:8]), T.tokv[:, 0:128]))
+        need("v", x, v_do)
+        x = v(V.tensor_copy(B("dp")[:], B("wn")[:, 0:CK].indirect(T.do[:, 0:6])))
+        need("v", x)
+        need("v", v(V.transpose(B("tw")[:], B("dp")[:])))
+        for a, e in enumerate(sorted(X[h])):
+            k = 3 * where[e][1]
+            x = tt(B("yl")[0:32, k:k + 3], B("tw")[32 * a:32 * a + 32, 0:96:32], B("tw")[32 * a:32 * a + 32, 16:96:32], A.add)
+        need("v", x)
+        for a in range(4):
+            v_of[h] = v(V.tensor_copy(B("of")[32 * a:32 * a + 32, :], B("yl")[0:32, :]))
 
-    v_of, v_ob = [None, None], [None, None]
+    gat = lambda h, k: (T["xg%d" % h][:, k:4 * W4:4], T.xp[:, 256 * k:256 * k + 256].indirect(T["of%d" % h][:, 0:12]))
+    s_g = [None, None]
 
-    def pick(h, qbuf, cbuf):
-        xg, of = T["xg%d" % h], T["of%d" % h]
-        need("v", ("lo%d" % h, 128))
-        v_ob[h] = tt(T["ob%d" % h][:], T["la%d" % h][:], T["lb%d" % h][:], A.add)
-        need("v", v_ob[h])
-        v_of[h] = ts(of[:], T["ob%d" % h][:], 1.0, None, A.mult)
-        gat = lambda k: (xg[:, k:4 * W4:4], T.xp[:, 256 * k:256 * k + 256].indirect(of[:, 0:12]))
+    def pick_s(h):
         need("s", s_xp, v_xp, v_of[h])
-        need("v", s_xp, v_xp, v_of[h])
         for k in (0, 1):
-            s_g = s(S.activation(*gat(k), F.Copy))
+            s_g[h] = s(S.activation(*gat(h, k), F.Copy))
+
+    def pick_v(h):
+        need("v", s_xp, v_xp, v_of[h])
         for k in (2, 3):
-            v_g = v(V.tensor_copy(*gat(k)))
-        need("v", s_g, v_g)
-        return v(V.quantize_mx(qbuf, cbuf, xg[:, 0:4 * W4]))
+            x = v(V.tensor_copy(*gat(h, k)))
+        return x
 
     ls = [0]
+    far_m = {z: [far_e[2 * k:2 * k + 2] for k in range(4)] for z in "qc"}
+    near_m = {"q": [near_e[0:4], near_e[4:8], far_e[0:4]], "c": [far_e[4:8], near_e[0:4], near_e[4:8]]}
+    AF, RF = ("af", 16), ("rf", 16)
+    got = sum(len(near_m[z][near_of(d).index(rank)]) for d in others for z in "qc")
+    AN, RN = ("an", got), ("rn", got)
 
     def send(parts):
         for z in ("q", "c"):
             tr = []
             for d, src, a, dst, b, sem in parts:
                 rid, pid, _ = topo.addr(T.cores[d])
-                k, eng = (far.index(d), far_e) if d in far else (others.index(d), near_e)
+                eng = far_m[z][far.index(d)] if d in far else near_m[z][others.index(d)]
                 sa, da = T[src + z][:, a:a + CK], T[dst + z][:, b:b + CK]
                 if z == "q":
                     sa, da = sa.bitcast(dt.uint8), da.bitcast(dt.uint8)
-                tr.append(RemoteDMATransfer(dst_ids=[DstId(rid=rid, pnc=pid)], dma_engine_mask=(1 << eng[2 * k]) | (1 << eng[2 * k + 1]),
+                tr.append(RemoteDMATransfer(dst_ids=[DstId(rid=rid, pnc=pid)], dma_engine_mask=sum(1 << e for e in eng),
                                             remote_sem=T.sem[sem], src=sa, dst=da))
-                ls[0] += 2
+                ls[0] += len(eng)
             g.remote_dma_fused(tr, local_sem=T.sem.ls)
 
     in_far = lambda d: CK * far_of(d).index(rank)
     in_near = lambda d: CK * near_of(d).index(rank)
 
-    def dispatch(h):
-        src = "t" if kind[h] == "far" else "n"
-        x = pick(h, T[src + "q"][:, 0:W4], T[src + "c"][:, 0:W4])
+    def dispatch(h, x):
+        src = "tn"[h]
+        need("v", x, s_g[h])
+        x = v(V.quantize_mx(T[src + "q"][:, 0:W4], T[src + "c"][:, 0:W4], T["xg%d" % h][:, 0:4 * W4]))
         need("p", x)
-        if kind[h] == "far":
+        if h == 0:
             send([(d, "t", CK * k, "n", 336 + in_far(d), "af") for k, d in enumerate(far)])
         else:
             send([(d, "n", CK * k, "n", W4 + in_near(d), "an") for k, d in enumerate(others)])
         return x
 
-    table = T.pl[:, 384:640]
-    v_chain = [None, None]
+    score(0)
+    for k in (2, 3):
+        v_xp = v(V.tensor_copy(*plane(k)))
+    need("s", DX)
+    s(S.activation(*plane(0), F.Copy))
+    own(0)
+    need("v", s_gt1)
+    v_gq[1] = v(V.quantize_mx(T.gq1[:, 0:128], T.gc1[:, 0:128], T.gt1[:, 0:512]))
+    score(1)
+    signs(0, SB[0])
+    sums(0, SB[0])
+    equal(0)
+    x = compare(0)
+    own(1)
+    total(0, x)
+    s_xp = s(S.activation(*plane(1), F.Copy))
+    signs(1, SB[1])
+    sums(1, SB[1][:1])
+    invert(0)
+    pick_s(0)
+    sums(1, SB[1][1:])
+    dispatch(0, pick_v(0))
+    equal(1)
+    v_read = compare(1)
+    total(1, v_read)
+    invert(1)
+    pick_s(1)
+    v_near = dispatch(1, pick_v(1))
 
-    def chain(h):
-        need("v", v_ob[h])
-        for m in range(3):
-            x = ts(T["ol%d" % h][:, m:16:4], T["ob%d" % h][:, m:12:3], 1.0, None, A.mult)
-        need("v", x, v_fresh, p_id)
-        for e in sorted(X[h]):
-            a = where[e][1]
+    table = T.pl[:, 384:640]
+
+    def chain(experts):
+        x = None
+        for e in experts:
+            h, a = where[e]
             at = table.indirect(T["ol%d" % h][:, 4 * a:4 * a + 3])
             o = W4 * h + CK * a
             if e == 0:
@@ -246,65 +280,65 @@ def rank_program(g, core, T, topo):
             need("v", x)
             x = v(V.tensor_copy(at, T.idr[:, CK * e:CK * e + CK]))
             need("v", x)
-        v_chain[h] = x
+        return x
 
-    score(0)
-    count(0)
-    score(1)
-    for k in (1, 2):
-        s_xp = s(S.activation(*plane(k), F.Copy))
-    invert(0, ["y"])
-    count(1)
-    invert(1, ["y", "s"])
-    v_x = [dispatch(0), None]
-    need("v", DW)
-    v_wq = v(V.quantize_mx(T.wq[:, 0:512], T.wc[:, 0:512], T.w1s[:, 0:2048]))
-    v_fresh = v(V.memset(table, 0.0))
-    v_x[1] = dispatch(1)
-    chain(0)
-    chain(1)
-    need("v", p_z)
-    for b in range(4):
-        v_ebq = v(V.quantize_mx(T.eq[:, 128 * b:128 * b + 128], T.ec[:, 128 * b:128 * b + 128], T.z[:, 3 - b:515 - b]))
-
-    def addresses():
-        need("v", v_q12)
+    def addresses(v_chain):
         for k in range(4):
-            v_mk = ts(T.mk[:, k:k + 1], T.q12[:], float(4 * k), None, A.is_equal)
+            v_mk = ts(T.mk[:, k:k + 1], p12, float(4 * k), None, A.is_equal)
         v(V.memset(T.pb[:, 0:16], 0.0))
-        need("s", v_chain[1], v_mk)
+        need("s", v_chain, v_mk)
         dg = [T["dg%d" % k] for k in range(4)]
-        for k in range(4):
-            s_dg = s(S.activation(dg[k][:], T.pl[:, k:640:4], F.Identity, scale=T.mk[:, k:k + 1]))
-        need("v", s_dg)
+        s_dg = [s(S.activation(dg[k][:], T.pl[:, k:640:4], F.Identity, scale=T.mk[:, k:k + 1])) for k in range(4)]
+        need("v", p_z)
+        for b in range(4):
+            v_eb = v(V.quantize_mx(T.eq[:, 128 * b:128 * b + 128], T.ec[:, 128 * b:128 * b + 128], T.z[:, 3 - b:515 - b]))
+        need("v", s_dg[1])
         tt(T.d01[:], dg[0][:], dg[1][:], A.add)
+        need("v", s_dg[3])
         need("v", tt(T.d23[:], dg[2][:], dg[3][:], A.add))
         need("v", tt(T.dd[:], T.d01[:], T.d23[:], A.add))
-        return ts(T.op[:], T.dd[:], T.p3f[:, 0:1], None, A.add)
+        return v_eb, ts(T.op[:], T.dd[:], p3, None, A.add)
 
-    def expert():
-        need("t", v_wq, v_x[kind.index("near")], ("an", 12), ("af", 16))
-        W8 = 2 * W4
-        tm = [t(PE.matmul_mx(T["ps%d" % i][:, 0:W8], T.wq[:, 128 * i:128 * i + 128], T.wc[:, 128 * i:128 * i + 128],
-                             T.nq[:, 144:528], T["nc"][:, 144:528], True, True)) for i in range(4)]
+    def expert(h, ready):
+        a, banks, hh = (336, 144)[h], [4 * h + i for i in range(4)], T["hh%d" % h]
+        need("t", v_wq, *ready)
+        tm = [t(PE.matmul_mx(T["ps%d" % k][:, 0:W4], T.wq[:, 128 * i:128 * i + 128], T.wc[:, 128 * i:128 * i + 128],
+                             T.nq[:, a:a + W4], T["nc"][:, a:a + W4], True, True)) for i, k in enumerate(banks)]
         for i in (0, 2):
             need("s", tm[i])
-            s_r = s(S.activation(T.hh[:, i:4 * W8:4], T["ps%d" % i][:, 0:W8], F.Relu, scale=0.05))
+            s_r = s(S.activation(hh[:, i:4 * W4:4], T["ps%d" % banks[i]][:, 0:W4], F.Relu, scale=0.05))
             need("v", tm[i + 1])
-            v_r = ts(T.hh[:, i + 1:4 * W8:4], T["ps%d" % (i + 1)][:, 0:W8], 0.0, 0.05, A.max, A.mult)
+            v_r = ts(hh[:, i + 1:4 * W4:4], T["ps%d" % banks[i + 1]][:, 0:W4], 0.0, 0.05, A.max, A.mult)
         need("v", s_r, v_r)
-        x = v(V.quantize_mx(T.mq[:, 144:528], T.mc[:, 144:528], T.hh[:, 0:4 * W8]))
+        x = v(V.quantize_mx(T.mq[:, a:a + W4], T.mc[:, a:a + W4], hh[:, 0:4 * W4]))
         need("p", x)
-        send([(d, "m", 336 + CK * k, "m", 528 + in_far(d), "rf") for k, d in enumerate(far)]
-             + [(d, "m", W4 + CK * k, "m", in_near(d), "rn") for k, d in enumerate(others)])
-        return x, [s_r, v_r]
+        if h == 0:
+            send([(d, "m", 336 + CK * k, "m", 528 + in_far(d), "rf") for k, d in enumerate(far)])
+        else:
+            send([(d, "m", W4 + CK * k, "m", in_near(d), "rn") for k, d in enumerate(others)])
+        return [s_r, v_r, x]
 
-    v_h, free = expert()
-    v_op = addresses()
+    need("v", DW)
+    v_wq = v(V.quantize_mx(T.wq[:, 0:512], T.wc[:, 0:512], T.w1s[:, 0:2048]))
+    v(V.memset(table, 0.0))
+    for h in range(2):
+        for m in range(3):
+            x = v(V.tensor_copy(T["ol%d" % h][:, m:16:4], T["of%d" % h][:, m:12:3]))
+    need("v", x, p_id)
+    chain(range(0, 4))
+    free = [expert(0, [AF]), None]
+    free[1] = expert(1, [AN, v_near, v_read, s_rk[1]])
+    v_eb, v_op = addresses(chain(range(4, 8)))
 
-    def unpack(pieces, banks, qv, cv, ready):
-        need("t", v_ebq, *ready)
-        tm = [t(PE.matmul_mx(T["ps%d" % k][:, 0:W4], T.eq[:, 128 * b:128 * b + 128], T.ec[:, 128 * b:128 * b + 128], qv, cv, True, True)) for b, k in enumerate(banks)]
+    def unpack(h):
+        ds, banks, a = T["ds%d" % h], [4 * h + i for i in range(4)], (528, 0)[h]
+        pieces = [(0, W4, ds, 0)]
+        if 0 in X[h]:
+            z = CK * where[0][1]
+            pieces = [(z, z + CK, T.pb, 4)] + [(lo, hi, ds, lo) for lo, hi in ((0, z), (z + CK, W4)) if lo < hi]
+        need("t", v_eb, (RF, RN)[h], *free[h])
+        tm = [t(PE.matmul_mx(T["ps%d" % k][:, 0:W4], T.eq[:, 128 * b:128 * b + 128], T.ec[:, 128 * b:128 * b + 128],
+                             T.mq[:, a:a + W4], T.mc[:, a:a + W4], True, True)) for b, k in enumerate(banks)]
         for b in (0, 2):
             for q, f in (("s", b), ("v", b + 1)):
                 need(q, tm[f])
@@ -316,23 +350,23 @@ def rank_program(g, core, T, topo):
                         v_r = v(V.tensor_copy(o, i))
         return [s_r, v_r]
 
-    for c in range(2):
-        ds = T["ds%d" % c]
-        pieces = [(0, W4, ds, 0)]
-        if c == 0:
-            z = CK * where[0][1]
-            pieces = [(z, z + CK, T.pb, 4)] + [(lo, hi, ds, lo) for lo, hi in ((0, z), (z + CK, W4)) if lo < hi]
-        if kind[c] == "far":
-            ready = unpack(pieces, [0, 1, 2, 3], T.mq[:, 528:720], T.mc[:, 528:720], [("rf", 16)] + free)
-        else:
-            ready = unpack(pieces, [4, 5, 6, 7], T.mq[:, 0:W4], T.mc[:, 0:W4], [("rn", 12), v_h, v_svread[1], s_cnt[1]])
+    def add(h, ready):
         need("v", v_op, *ready)
-        for e in sorted(X[c]):
+        for e in sorted(X[h]):
             if e == 0:
                 continue
-            d, o, k = W4 * where[e][1], 16 + W4 * e, 48 * c + 12 * where[e][1]
-            x = tt(T.pb[:, o:o + W4], T.pb[:, 0:o].indirect(T.op[:, k:k + 12]), ds[:, d:d + W4], A.add)
+            d, o, k = W4 * where[e][1], 16 + W4 * e, 48 * h + 12 * where[e][1]
+            x = tt(T.pb[:, o:o + W4], T.pb[:, 0:o].indirect(T.op[:, k:k + 12]), T["ds%d" % h][:, d:d + W4], A.add)
             need("v", x)
+        return x
+
+    if 0 in far:
+        add(0, unpack(0))
+        x = add(1, unpack(1))
+    else:
+        ready = unpack(0)
+        add(1, unpack(1))
+        x = add(0, ready)
     win = T.pb[:, 0:16 + N * W4]
     need("s", x)
     s_y = s(S.activation(T.yt[:, 512:1024], win.indirect(T.op[:, 128:160]), F.Copy))
@@ -342,5 +376,5 @@ def rank_program(g, core, T, topo):
     need("s", s_y)
     g.scalar.dma_start(T.y[:, 512:1024], T.yt[:, 512:1024]).then_inc(T.sem.dy, 16)
 
-    need("p", ("ls", ls[0]), ("dwg", 16), DX, DW, ("lo0", 128), ("lo1", 128), ("af", 16), ("an", 12), ("rf", 16), ("rn", 12), ("dy", 32))
+    need("p", ("ls", ls[0]), DWG, DX, DW, AF, AN, RF, RN, ("dy", 32))
     need("p", *[(q, cnt[q]) for q in ("v", "s", "t", "p")])

@@ -6,6 +6,10 @@ W4 = 4 * CK
 SB = [[5, 6, 7], [3, 4, 5, 6, 7]]
 SW = 257
 
+CALLS = [[("q", [0], False), ("c", [0, 1], False), ("q", [1], False)], [("q", [2], True), ("c", [2, 3], True), ("q", [3], False)]]
+STEPS = [(1, "f", 3, "n", 8), (4, "f", "n", 8), (6, "n", "f", 8), (6, "n", "f", 8)]
+HOLD = [e in (2, 6, 7) for e in range(8)]
+
 SCRATCH = {}
 
 
@@ -16,18 +20,18 @@ def _sbuf(dtype, names):
             SCRATCH[m] = ("sbuf", [128, int(c)], dtype)
 
 
-_sbuf("bfloat16", "wgs:32 xs:1024 xp:1024 w1s:2048 ones:516 z:516 col:256 blk:256 tok0:128 tokv:128 hh@:768 gt@:512 cmp@:2048 cs@:1024 sg@:%d "
+_sbuf("bfloat16", "wgs:32 xs:1024 xp:1024 w1s:2048 ones:128 z:516 col:256 blk:256 tok0:128 tokv:128 hh@:768 gt@:512 cmp@:2048 cs@:1024 sg@:%d "
       "rk@:8 eqb@:256 es@:256 wn@:256 dp@:96 tw@:96 yl@:12 xg@:768" % (8 * SW))
 for _d, _s in (("float8_e4m3fn_x4", "q"), ("uint8", "c")):
     _sbuf(_d, " ".join("%s%s%s" % (w[0], _s, w[1:]) for w in "x:256 w:512 e:512 t:192 n:528 m:720 g@:128".split()))
 _sbuf("int32", "ic:1 pi:5")
 _sbuf("float32", "e4:64 pf:5 do0:6 mk:4 idr:384 pl:640 dg0:160 dg1:160 dg2:160 dg3:160 d01:160 d23:160 dd:160")
-_sbuf("float32", "ds@:768 pb:%d yt:1024 tt@:256 ac@:16" % (16 + 8 * W4))
+_sbuf("float32", "ds@:768 pb:%d yt:1024 tt@:256 ac@:24" % (16 + 8 * W4))
 _sbuf("uint16", "go:64 do:6 op:160 ru@:8 ol@:16 of@:12")
 for _b in range(8):
     SCRATCH["ps%d" % _b] = ("psum", [128, 512], "float32")
 
-SEMAPHORES = ["v", "t", "s", "p", "dwg", "dx", "dw", "af", "an", "rf", "rn", "ls", "dy"]
+SEMAPHORES = ["v", "t", "s", "p", "dwg", "dx", "dw", "af", "an", "rf0", "rf1", "rf2", "rf3", "rn", "ls", "dy"]
 
 
 def rank_program(g, core, T, topo):
@@ -73,17 +77,20 @@ def rank_program(g, core, T, topo):
 
     imp = dict(allow_small_or_imprecise_dtypes=True)
     p_ic = p(g.iota(T.ic[:], [[0, 1]], 0, 1))
-    for h in range(2):
-        p_e4 = p(g.iota(T.e4[:, 32 * h:32 * h + 32], [[4, 4], [0, 8]], 4 * min(X[h]), 0, **imp))
-    p_tok = p(g.iota(T.tok0[:], [[32, 8], [1, 16]], 0, 0, **imp))
+    p_e4 = p(g.iota(T.e4[:], [[4, N], [0, 8]], 0, 0, **imp))
     p_do = p(g.iota(T.do0[:], [[16, 3], [0, 2]], 0, 0, **imp))
+    v(V.memset(T.ones[:], 1.0))
+    need("p", v(V.memset(T.z[:], 0.0)))
+    p_z = p(g.affine_select(T.z[:, 3:515:4], T.ones[:], [[-1, 128]], A.is_equal, 0.0, 0, 1))
     p_col = p(g.iota(T.col[:], [[0, 8], [1, 32]], 0, 0, **imp))
+    p_tok = p(g.iota(T.tok0[:], [[32, 8], [1, 16]], 0, 0, **imp))
     for h in range(2):
         p_m = p(g.iota(T["sg%d" % h][:, SW - 1:8 * SW:SW], [[-32, 8]], -32, 0, **imp))
-    p_wn = [p(g.iota(T["wn%d" % h][:, 0:CK], [[0, CK]], 0, 0, **imp)) for h in range(2)]
-    v_ones = v(V.memset(T.ones[:], 1.0))
-    need("p", v_ones)
-    p_z = p(g.affine_select(T.z[:], T.ones[:], [[-1, 516]], A.is_equal, 0.0, 3, 4))
+    zero = lambda ap, n: p(g.iota(ap, [[0, n]], 0, 0, **imp))
+    p_wn = [zero(T["wn%d" % h][:, 0:CK], CK) for h in range(2)]
+    zero(T.pl[:, 384:640], 256)
+    zero(T.pl[:, W4 * where[0][0] + CK * where[0][1]:W4 * where[0][0] + CK * where[0][1] + CK], CK)
+    zero(T.pb[:, 0:16], 16)
     p_id = p(g.iota(T.idr[:], [[W4, N], [4, CK]], 16, 0, **imp))
 
     need("v", p_ic)
@@ -92,20 +99,25 @@ def rank_program(g, core, T, topo):
     need("v", x)
     v_pf = v(V.tensor_copy(T.pf[:], T.pi[:]))
     p3, p31, p16, p15, p12 = [T.pf[:, k:k + 1] for k in range(5)]
-    need("v", v_pf, p_e4)
+    need("v", v_pf, p_e4, p_do)
     v_go = ts(T.go[:], T.e4[:], p3, None, A.add)
-    need("v", p_tok, p_do)
-    v_tok = ts(T.tokv[:], T.tok0[:], p16, None, A.add)
     v_do = ts(T.do[:], T.do0[:], p15, None, A.add)
-    need("v", DWG, v_go)
-    v_gt = v(V.tensor_copy(T.gt0[:, 0:256], T.wgs[:, 0:32].indirect(T.go[:, 0:16])))
-    need("s", DWG, v_go)
-    s_gt0 = s(S.activation(T.gt0[:, 256:512], T.wgs[:, 0:32].indirect(T.go[:, 16:32]), F.Copy))
-    s_gt1 = s(S.activation(T.gt1[:], T.wgs[:, 0:32].indirect(T.go[:, 32:64]), F.Copy))
-    need("v", v_gt, s_gt0)
-    v_gq = [v(V.quantize_mx(T.gq0[:, 0:128], T.gc0[:, 0:128], T.gt0[:, 0:512])), None]
+    for k in range(4):
+        v_mk = ts(T.mk[:, k:k + 1], p12, float(4 * k), None, A.is_equal)
+    need("v", p_z)
+    for b in range(4):
+        v_eb = v(V.quantize_mx(T.eq[:, 128 * b:128 * b + 128], T.ec[:, 128 * b:128 * b + 128], T.z[:, 3 - b:515 - b]))
     need("v", p_col)
     v_blk = ts(T.blk[:], T.col[:], p31, None, A.not_equal)
+    need("v", DWG, v_go)
+    gate = lambda h, a, b: (T["gt%d" % h][:, 16 * a:16 * b], T.wgs[:, 0:32].indirect(T.go[:, 8 * min(X[h]) + a:8 * min(X[h]) + b]))
+    v_gt = v(V.tensor_copy(*gate(0, 0, 16)))
+    need("s", DWG, v_go)
+    s_gt0 = s(S.activation(*gate(0, 16, 32), F.Copy))
+    s_gt1 = s(S.activation(*gate(1, 8, 32), F.Copy))
+    need("v", v_gt, s_gt0)
+    v_gq = [v(V.quantize_mx(T.gq0[:, 0:128], T.gc0[:, 0:128], T.gt0[:, 0:512])), None]
+    v_gt = v(V.tensor_copy(*gate(1, 0, 8)))
 
     need("v", DX)
     v_xq = v(V.quantize_mx(T.xq[:, 0:256], T.xc[:, 0:256], T.xs[:, 0:1024]))
@@ -122,15 +134,15 @@ def rank_program(g, core, T, topo):
     v_own, v_es, v_e, v_rk, s_rk, s_sg = [None, None], [None, None], [None, None], [None, None], [None, None], [{}, {}]
     slot = lambda h, b: T["cs%d" % h][:, 128 * b + 127:128 * b + 128]
 
-    def own(h):
+    def own(h, a, b):
         need("v", t_sv[h])
-        v_own[h] = v(V.transpose(T["tt%d" % h][:], sv[h][:, 0:256]))
+        v_own[h] = v(V.transpose(T["tt%d" % h][:, 32 * a:32 * b], sv[h][:, 32 * a:32 * b]))
 
     def equal(h):
         need("v", v_own[h])
         x = tt(T["eqb%d" % h][:], sv[h][:, 0:256], T["tt%d" % h][:], A.is_equal)
         need("v", x, v_blk)
-        v_es[h] = v(V.tensor_tensor_scan(T["es%d" % h][:], T.blk[:], T["eqb%d" % h][:], 0.0, A.mult, A.add))
+        v_es[h] = v(V.tensor_tensor_scan(T["es%d" % h][:], T.blk[:], T["eqb%d" % h][:], 0.0, A.mult, A.subtract))
 
     def compare(h):
         P, cm = sv[h], T["cmp%d" % h]
@@ -143,10 +155,10 @@ def rank_program(g, core, T, topo):
 
     def total(h, x):
         cm = T["cmp%d" % h]
-        need("v", x)
+        need("v", x, v_es[h])
         for b in range(8 - len(SB[h])):
             v_rk[h] = v(V.tensor_tensor_scan(T["cs%d" % h][:, 128 * b:128 * b + 128], cm[:, 256 * b:256 * b + 128], cm[:, 256 * b + 128:256 * b + 256],
-                                             0.0, A.add, A.add))
+                                             T["es%d" % h][:, 32 * b + 31:32 * b + 32], A.add, A.add))
 
     def signs(h, blocks):
         need("s", t_ss[h], v_own[h])
@@ -165,15 +177,19 @@ def rank_program(g, core, T, topo):
                 last[b] = s(S.activation(hi, hi, F.Relu, scale=-1.0, accum_out=ac[:, 8 + b:9 + b]))
         for b in blocks:
             need("s", last[b])
-            s_rk[h] = s(S.activation(slot(h, b), ac[:, b:b + 1], F.Identity, scale=-1.0, bias=ac[:, 8 + b:9 + b] if b < 7 else 256.0))
+            s_sg[h][b] = s(S.activation(ac[:, 16 + b:17 + b], ac[:, b:b + 1], F.Identity, scale=-1.0, bias=ac[:, 8 + b:9 + b] if b < 7 else 256.0))
+
+    def settle(h, blocks):
+        for b in blocks:
+            need("s", s_sg[h][b], v_es[h])
+            s_rk[h] = s(S.activation(slot(h, b), T["ac%d" % h][:, 16 + b:17 + b], F.Identity, bias=T["es%d" % h][:, 32 * b + 31:32 * b + 32]))
 
     v_of = [None, None]
 
     def invert(h):
         B = lambda n: T["%s%d" % (n, h)]
-        need("v", v_rk[h], s_rk[h], v_es[h])
-        need("v", tt(B("rk")[:], B("cs")[:, 127:1024:128], B("es")[:, 31:256:32], A.subtract))
-        x = v(V.tensor_copy(B("ru")[:], B("rk")[:]))
+        need("v", v_rk[h], s_rk[h])
+        x = v(V.tensor_copy(B("ru")[:], B("cs")[:, 127:1024:128]))
         need("v", x, v_tok, p_wn[h])
         x = v(V.tensor_copy(B("wn")[:, 0:256].indirect(B("ru")[:, 0:8]), T.tokv[:, 0:128]))
         need("v", x, v_do)
@@ -202,18 +218,20 @@ def rank_program(g, core, T, topo):
         return x
 
     ls = [0]
-    far_m = {z: [far_e[2 * k:2 * k + 2] for k in range(4)] for z in "qc"}
-    near_m = {"q": [near_e[0:4], near_e[4:8], far_e[0:4]], "c": [far_e[4:8], near_e[0:4], near_e[4:8]]}
-    AF, RF = ("af", 16), ("rf", 16)
-    got = sum(len(near_m[z][near_of(d).index(rank)]) for d in others for z in "qc")
-    AN, RN = ("an", got), ("rn", got)
+    near_m = {"q": [near_e[0:4], near_e[4:6], near_e[6:8]], "c": [near_e[4:8], near_e[0:2], near_e[2:4]]}
+    share = lambda ks, k: far_e[0::2][ks.index(k)::len(ks)]
+    masks = {"af": {z: [share(ks, k) for k in range(4) for y, ks, _ in CALLS[0] + CALLS[1] if z in y and k in ks] for z in "qc"}, "rf": {z: [far_e[2 * k:2 * k + 2] for k in range(4)] for z in "qc"},
+             "an": {z: [near_e[0:4], near_e[4:8], far_e[1::2]] for z in "qc"}, "rn": near_m}
+    mine = lambda n, d: sum(len(masks[n][z][(far_of(d) if d in far else near_of(d)).index(rank)]) for z in "qc")
+    AF, AN, RN = [(n, sum(mine(n, d) for d in ds)) for n, ds in (("af", far), ("an", others), ("rn", others))]
+    RF = [("rf%d" % k, mine("rf", d)) for k, d in enumerate(far)]
 
-    def send(parts):
-        for z in ("q", "c"):
+    def send(parts, kinds="qc"):
+        for z in kinds:
             tr = []
             for d, src, a, dst, b, sem in parts:
                 rid, pid, _ = topo.addr(T.cores[d])
-                eng = far_m[z][far.index(d)] if d in far else near_m[z][others.index(d)]
+                eng = masks[sem[:2]][z][(far if d in far else others).index(d)]
                 sa, da = T[src + z][:, a:a + CK], T[dst + z][:, b:b + CK]
                 if z == "q":
                     sa, da = sa.bitcast(dt.uint8), da.bitcast(dt.uint8)
@@ -230,35 +248,39 @@ def rank_program(g, core, T, topo):
         need("v", x, s_g[h])
         x = v(V.quantize_mx(T[src + "q"][:, 0:W4], T[src + "c"][:, 0:W4], T["xg%d" % h][:, 0:4 * W4]))
         need("p", x)
-        if h == 0:
-            send([(d, "t", CK * k, "n", 336 + in_far(d), "af") for k, d in enumerate(far)])
-        else:
-            send([(d, "n", CK * k, "n", W4 + in_near(d), "an") for k, d in enumerate(others)])
+        for z, ks, near in CALLS[h]:
+            send([(far[k], "t", CK * k, "n", 336 + in_far(far[k]), "af") for k in ks]
+                 + [(d, "n", CK * k, "n", W4 + in_near(d), "an") for k, d in enumerate(others) if near], z)
         return x
 
     score(0)
+    need("v", s_gt1, v_gt)
+    v_gq[1] = v(V.quantize_mx(T.gq1[:, 0:128], T.gc1[:, 0:128], T.gt1[:, 0:512]))
+    score(1)
     for k in (2, 3):
         v_xp = v(V.tensor_copy(*plane(k)))
     need("s", DX)
-    s(S.activation(*plane(0), F.Copy))
-    own(0)
-    need("v", s_gt1)
-    v_gq[1] = v(V.quantize_mx(T.gq1[:, 0:128], T.gc1[:, 0:128], T.gt1[:, 0:512]))
-    score(1)
+    for k in (0, 1):
+        s_xp = s(S.activation(*plane(k), F.Copy))
+    own(0, 0, 8)
     signs(0, SB[0])
-    sums(0, SB[0])
     equal(0)
+    sums(0, SB[0])
+    settle(0, SB[0])
+    need("s", p_tok, v_pf)
+    v_tok = s(S.activation(T.tokv[:], T.tok0[:], F.Identity, bias=p16))
     x = compare(0)
-    own(1)
+    own(1, SB[1][0], 8)
     total(0, x)
-    s_xp = s(S.activation(*plane(1), F.Copy))
     signs(1, SB[1])
     sums(1, SB[1][:1])
     invert(0)
     pick_s(0)
     sums(1, SB[1][1:])
     dispatch(0, pick_v(0))
+    own(1, 0, SB[1][0])
     equal(1)
+    settle(1, SB[1])
     v_read = compare(1)
     total(1, v_read)
     invert(1)
@@ -267,37 +289,28 @@ def rank_program(g, core, T, topo):
 
     table = T.pl[:, 384:640]
 
-    def chain(experts):
-        x = None
-        for e in experts:
+    v_chain = []
+
+    def chain(upto):
+        for e in range(len(v_chain), upto):
             h, a = where[e]
-            at = table.indirect(T["ol%d" % h][:, 4 * a:4 * a + 3])
+            at = table.indirect(T["ol%d" % h][:, 3 * a - 3:3 * a] if a % 2 else T["of%d" % h][:, 3 * a:3 * a + 3])
             o = W4 * h + CK * a
-            if e == 0:
-                x = v(V.memset(T.pl[:, o:o + CK], 0.0))
-            else:
-                x = v(V.tensor_copy(T.pl[:, o:o + CK], at))
-            need("v", x)
-            x = v(V.tensor_copy(at, T.idr[:, CK * e:CK * e + CK]))
-            need("v", x)
-        return x
+            if e:
+                need("v", v(V.tensor_copy(T.pl[:, o:o + CK], at)))
+            v_chain.append(v(V.tensor_copy(at, T.idr[:, CK * e:CK * e + CK])))
+            need("v", v_chain[-1])
 
     def addresses(v_chain):
-        for k in range(4):
-            v_mk = ts(T.mk[:, k:k + 1], p12, float(4 * k), None, A.is_equal)
-        v(V.memset(T.pb[:, 0:16], 0.0))
         need("s", v_chain, v_mk)
         dg = [T["dg%d" % k] for k in range(4)]
         s_dg = [s(S.activation(dg[k][:], T.pl[:, k:640:4], F.Identity, scale=T.mk[:, k:k + 1])) for k in range(4)]
-        need("v", p_z)
-        for b in range(4):
-            v_eb = v(V.quantize_mx(T.eq[:, 128 * b:128 * b + 128], T.ec[:, 128 * b:128 * b + 128], T.z[:, 3 - b:515 - b]))
         need("v", s_dg[1])
         tt(T.d01[:], dg[0][:], dg[1][:], A.add)
         need("v", s_dg[3])
         need("v", tt(T.d23[:], dg[2][:], dg[3][:], A.add))
         need("v", tt(T.dd[:], T.d01[:], T.d23[:], A.add))
-        return v_eb, ts(T.op[:], T.dd[:], p3, None, A.add)
+        return ts(T.op[:], T.dd[:], p3, None, A.add)
 
     def expert(h, ready):
         a, banks, hh = (336, 144)[h], [4 * h + i for i in range(4)], T["hh%d" % h]
@@ -311,70 +324,84 @@ def rank_program(g, core, T, topo):
             v_r = ts(hh[:, i + 1:4 * W4:4], T["ps%d" % banks[i + 1]][:, 0:W4], 0.0, 0.05, A.max, A.mult)
         need("v", s_r, v_r)
         x = v(V.quantize_mx(T.mq[:, a:a + W4], T.mc[:, a:a + W4], hh[:, 0:4 * W4]))
-        need("p", x)
-        if h == 0:
-            send([(d, "m", 336 + CK * k, "m", 528 + in_far(d), "rf") for k, d in enumerate(far)])
-        else:
-            send([(d, "m", W4 + CK * k, "m", in_near(d), "rn") for k, d in enumerate(others)])
+        back = [[(d, "m", 336 + CK * k, "m", 528 + in_far(d), "rf%d" % far_of(d).index(rank)) for k, d in enumerate(far)],
+                [(d, "m", W4 + CK * k, "m", in_near(d), "rn") for k, d in enumerate(others)]]
+        if not (HOLD[rank] and h):
+            need("p", x)
+            send(back[h] + (back[1] if HOLD[rank] else []))
         return [s_r, v_r, x]
 
     need("v", DW)
     v_wq = v(V.quantize_mx(T.wq[:, 0:512], T.wc[:, 0:512], T.w1s[:, 0:2048]))
-    v(V.memset(table, 0.0))
     for h in range(2):
-        for m in range(3):
-            x = v(V.tensor_copy(T["ol%d" % h][:, m:16:4], T["of%d" % h][:, m:12:3]))
+        x = v(V.tensor_copy(T["ol%d" % h][:, 0:9], T["of%d" % h][:, 3:12]))
     need("v", x, p_id)
-    chain(range(0, 4))
-    free = [expert(0, [AF]), None]
-    free[1] = expert(1, [AN, v_near, v_read, s_rk[1]])
-    v_eb, v_op = addresses(chain(range(4, 8)))
+    free = [None, None]
+    arrived = [[AF], [AN, v_near, v_read, s_rk[1]]]
+    place = sorted(X[1]).index(rank)
+    for step in STEPS[place]:
+        if step in ("f", "n"):
+            free["fn".index(step)] = expert("fn".index(step), arrived["fn".index(step)])
+        else:
+            chain(step)
+    v_op = addresses(v_chain[-1])
 
-    def unpack(h):
-        ds, banks, a = T["ds%d" % h], [4 * h + i for i in range(4)], (528, 0)[h]
-        pieces = [(0, W4, ds, 0)]
-        if 0 in X[h]:
-            z = CK * where[0][1]
-            pieces = [(z, z + CK, T.pb, 4)] + [(lo, hi, ds, lo) for lo, hi in ((0, z), (z + CK, W4)) if lo < hi]
-        need("t", v_eb, (RF, RN)[h], *free[h])
-        tm = [t(PE.matmul_mx(T["ps%d" % k][:, 0:W4], T.eq[:, 128 * b:128 * b + 128], T.ec[:, 128 * b:128 * b + 128],
-                             T.mq[:, a:a + W4], T.mc[:, a:a + W4], True, True)) for b, k in enumerate(banks)]
-        for b in (0, 2):
-            for q, f in (("s", b), ("v", b + 1)):
-                need(q, tm[f])
-                for lo, hi, buf, at in pieces:
-                    o, i = buf[:, 4 * at + f:4 * (at + hi - lo):4], T["ps%d" % banks[f]][:, lo:hi]
-                    if q == "s":
-                        s_r = s(S.activation(o, i, F.Copy))
-                    else:
-                        v_r = v(V.tensor_copy(o, i))
-        return [s_r, v_r]
+    banks = [free[0] + free[1], free[0] + free[1]]
+    turn = [0]
 
-    def add(h, ready):
-        need("v", v_op, *ready)
-        for e in sorted(X[h]):
-            if e == 0:
-                continue
-            d, o, k = W4 * where[e][1], 16 + W4 * e, 48 * h + 12 * where[e][1]
-            x = tt(T.pb[:, o:o + W4], T.pb[:, 0:o].indirect(T.op[:, k:k + 12]), T["ds%d" % h][:, d:d + W4], A.add)
+    def unpack(a, n, arrived):
+        k = turn[0] % 2
+        turn[0] += 1
+        need("t", v_eb, arrived, *banks[k])
+        return k, [t(PE.matmul_mx(T["ps%d" % (4 * k + b)][:, 0:n], T.eq[:, 128 * b:128 * b + 128], T.ec[:, 128 * b:128 * b + 128],
+                                  T.mq[:, a:a + n], T.mc[:, a:a + n], True, True)) for b in range(4)]
+
+    def fetch(q, u, b, e, c, n, *ready):
+        h, a = where[e]
+        buf, at = (T.pb, 16) if e == 0 else (T["ds%d" % h], W4 * a)
+        o, i = buf[:, at + b:at + W4 * n:4], T["ps%d" % (4 * u[0] + b)][:, c:c + CK * n]
+        need(q, u[1][b], *ready)
+        return s(S.activation(o, i, F.Copy)) if q == "s" else v(V.tensor_copy(o, i))
+
+    ready, added = {}, [0]
+
+    def add(upto):
+        for e in range(added[0] + 1, upto + 1):
+            h, a = where[e]
+            need("v", v_op, *(ready.get(e, []) + ready[0]))
+            o, k = 16 + W4 * e, 48 * h + 12 * a
+            x = tt(T.pb[:, o:o + W4], T.pb[:, 0:o].indirect(T.op[:, k:k + 12]), T["ds%d" % h][:, W4 * a:W4 * a + W4], A.add)
             need("v", x)
+            added[0] = e
         return x
 
+    def far_in(k, queues):
+        u = unpack(528 + CK * (k + 1) - 128, 128, RF[k])
+        banks[u[0]] = ready[far[k]] = [fetch(queues[b % 2], u, b, far[k], 128 - CK, 1) for b in range(4)][-2:]
+
     if 0 in far:
-        add(0, unpack(0))
-        x = add(1, unpack(1))
+        for k in range(3):
+            far_in(k, "ss")
+        u = unpack(0, W4, RN)
+        banks[u[0]] = ready[4] = [fetch("s", u, b, X[1][0], 0, 4) for b in range(4)][-1:]
+        add(2)
     else:
-        ready = unpack(0)
-        add(1, unpack(1))
-        x = add(0, ready)
+        u = unpack(0, W4, RN)
+        first = [fetch("sv"[b % 2], u, b, e, CK * where[e][1], 1) for b in range(4) for e in (0, 1)]
+        ready[0] = first[-3:]
+        pair = min((2, 3), key=lambda e: where[e][1])
+        banks[u[0]] = ready[2] = [fetch("s", u, b, pair, CK * where[pair][1], 2, *first[-1:] * (b % 2)) for b in (0, 2, 1, 3)][-1:]
+        for k in range(3):
+            far_in(k, "ss")
+        add(6)
+    far_in(3, "sv")
+    x = add(7)
     win = T.pb[:, 0:16 + N * W4]
     need("s", x)
-    s_y = s(S.activation(T.yt[:, 512:1024], win.indirect(T.op[:, 128:160]), F.Copy))
-    v_y = v(V.tensor_copy(T.yt[:, 0:512], win.indirect(T.op[:, 96:128])))
-    need("y", v_y)
-    g.sync.dma_start(T.y[:, 0:512], T.yt[:, 0:512]).then_inc(T.sem.dy, 16)
-    need("s", s_y)
-    g.scalar.dma_start(T.y[:, 512:1024], T.yt[:, 512:1024]).then_inc(T.sem.dy, 16)
+    for a in (0, 512):
+        part = lambda c: (T.yt[:, c:c + 256], win.indirect(T.op[:, 96 + c // 16:112 + c // 16]))
+        need("y", v(V.tensor_copy(*part(a))), s(S.activation(*part(a + 256), F.Copy)))
+        g.sync.dma_start(T.y[:, a:a + 512], T.yt[:, a:a + 512]).then_inc(T.sem.dy, 16)
 
-    need("p", ("ls", ls[0]), DWG, DX, DW, AF, AN, RF, RN, ("dy", 32))
+    need("p", ("ls", ls[0]), DWG, DX, DW, AF, AN, *RF, RN, ("dy", 32))
     need("p", *[(q, cnt[q]) for q in ("v", "s", "t", "p")])

@@ -5,9 +5,11 @@ CK = 48
 W4 = 4 * CK
 SB = [[5, 6, 7], [3, 4, 5, 6, 7]]
 SW = 257
+W2 = 2 * CK
+HALF = 8 + 8 * W2
 
 CALLS = [[("q", [0], False), ("c", [0, 1], False), ("q", [1], False)], [("q", [2], True), ("c", [2, 3], True), ("q", [3], False)]]
-STEPS = [(1, "f", 3, "n", 8), (4, "f", "n", 8), (6, "n", "f", 8), (6, "n", "f", 8)]
+STEPS = [(5, "f", 2, "n", "m", "s", "a"), (7, "f", "n", "m", "s", "a"), (7, "m", "n", "f", "s", "a"), (7, "m", "n", "f", "s", "a")]
 HOLD = [e in (2, 6, 7) for e in range(8)]
 
 SCRATCH = {}
@@ -21,13 +23,13 @@ def _sbuf(dtype, names):
 
 
 _sbuf("bfloat16", "wgs:32 xs:1024 xp:1024 w1s:2048 ones:128 z:516 col:256 blk:256 tok0:128 tokv:128 hh@:768 gt@:512 cmp@:2048 cs@:1024 sg@:%d "
-      "rk@:8 eqb@:256 es@:256 wn@:256 dp@:96 tw@:96 yl@:12 xg@:768" % (8 * SW))
+      "eqb@:256 es@:256 wn@:256 dp@:96 tw@:96 yl@:12 xg@:768" % (8 * SW))
 for _d, _s in (("float8_e4m3fn_x4", "q"), ("uint8", "c")):
     _sbuf(_d, " ".join("%s%s%s" % (w[0], _s, w[1:]) for w in "x:256 w:512 e:512 t:192 n:528 m:720 g@:128".split()))
-_sbuf("int32", "ic:1 pi:5")
-_sbuf("float32", "e4:64 pf:5 do0:6 mk:4 idr:384 pl:640 dg0:160 dg1:160 dg2:160 dg3:160 d01:160 d23:160 dd:160")
-_sbuf("float32", "ds@:768 pb:%d yt:1024 tt@:256 ac@:24" % (16 + 8 * W4))
-_sbuf("uint16", "go:64 do:6 op:160 ru@:8 ol@:16 of@:12")
+_sbuf("int32", "ic:1 pi:8")
+_sbuf("float32", "e4:64 pf:9 do0:6 mk:12 idr:384 pl:640 lk:384 old:192 tb@:256 dg:640 keep:640 dd:640")
+_sbuf("float32", "ds@:768 pb:%d yt:1024 tt@:256 ac@:24" % (2 * HALF))
+_sbuf("uint16", "go:64 do:6 op:112 ru@:8 ol@:10 of@:12")
 for _b in range(8):
     SCRATCH["ps%d" % _b] = ("psum", [128, 512], "float32")
 
@@ -50,9 +52,10 @@ def rank_program(g, core, T, topo):
     Q = {"v": g.vector, "t": g.tensor, "s": g.scalar, "p": g, "y": g.sync}
     cnt = {"v": 0, "t": 0, "s": 0, "p": 0}
     seen = {}
+    D = {}
 
     def need(q, *toks):
-        for s, n in toks:
+        for s, n in [D[k] if k in D else k for k in toks]:
             if seen.get((q, s), 0) < n:
                 Q[q].wait_ge(T.sem[s], n)
                 seen[(q, s)] = n
@@ -62,6 +65,12 @@ def rank_program(g, core, T, topo):
         cnt[q] += 1
         return (q, cnt[q])
 
+    def weave(steps, fill):
+        for step in steps:
+            step()
+            if fill:
+                fill.pop(0)()
+
     V, S, PE = g.vector, g.scalar, g.tensor
     v = lambda ins: done("v", ins)
     s = lambda ins: done("s", ins)
@@ -69,6 +78,7 @@ def rank_program(g, core, T, topo):
     p = lambda ins: done("p", ins)
     ts = lambda out, in0, s1, s2, *ops: v(V.tensor_scalar(out, in0, s1, s2, *ops))
     tt = lambda out, a, b, op: v(V.tensor_tensor(out, a, b, op))
+    both = lambda *fs: lambda: [f() for f in fs]
 
     g.scalar.dma_start(T.wgs[:], T.wg[:, 0:32]).then_inc(T.sem.dwg, 16)
     g.sync.dma_start(T.xs[:], T.x[:]).then_inc(T.sem.dx, 16)
@@ -79,148 +89,120 @@ def rank_program(g, core, T, topo):
     p_ic = p(g.iota(T.ic[:], [[0, 1]], 0, 1))
     p_e4 = p(g.iota(T.e4[:], [[4, N], [0, 8]], 0, 0, **imp))
     p_do = p(g.iota(T.do0[:], [[16, 3], [0, 2]], 0, 0, **imp))
-    v(V.memset(T.ones[:], 1.0))
-    need("p", v(V.memset(T.z[:], 0.0)))
-    p_z = p(g.affine_select(T.z[:, 3:515:4], T.ones[:], [[-1, 128]], A.is_equal, 0.0, 0, 1))
     p_col = p(g.iota(T.col[:], [[0, 8], [1, 32]], 0, 0, **imp))
     p_tok = p(g.iota(T.tok0[:], [[32, 8], [1, 16]], 0, 0, **imp))
     for h in range(2):
         p_m = p(g.iota(T["sg%d" % h][:, SW - 1:8 * SW:SW], [[-32, 8]], -32, 0, **imp))
-    zero = lambda ap, n: p(g.iota(ap, [[0, n]], 0, 0, **imp))
-    p_wn = [zero(T["wn%d" % h][:, 0:CK], CK) for h in range(2)]
-    zero(T.pl[:, 384:640], 256)
-    zero(T.pl[:, W4 * where[0][0] + CK * where[0][1]:W4 * where[0][0] + CK * where[0][1] + CK], CK)
-    zero(T.pb[:, 0:16], 16)
-    p_id = p(g.iota(T.idr[:], [[W4, N], [4, CK]], 16, 0, **imp))
+    fill = lambda ap, n, c=0: p(g.iota(ap, [[0, n]], c, 0, **imp))
+    p_wn = [fill(T["wn%d" % h][:, 0:CK], CK) for h in range(2)]
+    v(V.memset(T.ones[:], 1.0))
+    need("p", v(V.memset(T.z[:], 0.0)))
+    p_z = p(g.affine_select(T.z[:, 3:515:4], T.ones[:], [[-1, 128]], A.is_equal, 0.0, 0, 1))
+    need("p", fill(T.keep[:], 640, 1))
+    fill(T.keep[:, 0:384:8], 48)
+    fill(T.keep[:, 384:640:4], 64)
+    for e, buf in ((0, T.pl), (4, T.lk)):
+        fill(T["tb%d" % where[e][0]][:], 256)
+        fill(buf[:, W4 * where[e][0] + CK * where[e][1]:W4 * where[e][0] + CK * where[e][1] + CK], CK)
+    for a in (0, HALF):
+        fill(T.pb[:, a:a + 8], 8)
+    p_id = p(g.iota(T.idr[:], [[W2, N], [2, CK]], 8, 0, **imp))
 
     need("v", p_ic)
-    for k, m in enumerate((3, 31, 16, 15, 12)):
+    for k, m in enumerate((3, 31, 16, 15, 12, 14, 1, 2)):
         x = ts(T.pi[:, k:k + 1], T.ic[:], m, None, A.bitwise_and)
     need("v", x)
-    v_pf = v(V.tensor_copy(T.pf[:], T.pi[:]))
-    p3, p31, p16, p15, p12 = [T.pf[:, k:k + 1] for k in range(5)]
+    v_pf = v(V.tensor_copy(T.pf[:, 0:8], T.pi[:]))
+    p3, p31, p16, p15, p12, p14, p1, p2, pc = [T.pf[:, k:k + 1] for k in range(9)]
     need("v", v_pf, p_e4, p_do)
     v_go = ts(T.go[:], T.e4[:], p3, None, A.add)
     v_do = ts(T.do[:], T.do0[:], p15, None, A.add)
-    for k in range(4):
-        v_mk = ts(T.mk[:, k:k + 1], p12, float(4 * k), None, A.is_equal)
-    need("v", p_z)
-    for b in range(4):
-        v_eb = v(V.quantize_mx(T.eq[:, 128 * b:128 * b + 128], T.ec[:, 128 * b:128 * b + 128], T.z[:, 3 - b:515 - b]))
+    ts(pc, p2, HALF / 2, p1, A.mult, A.add)
     need("v", p_col)
+    ts(T.mk[:, 0:8], T.col[:, 0:16:2], p14, None, A.is_equal)
+    v_mk = ts(T.mk[:, 8:12], T.col[:, 0:16:4], p12, None, A.is_equal)
     v_blk = ts(T.blk[:], T.col[:], p31, None, A.not_equal)
+    need("s", p_tok, v_pf)
+    v_tok = s(S.activation(T.tokv[:], T.tok0[:], F.Identity, bias=p16))
     need("v", DWG, v_go)
     gate = lambda h, a, b: (T["gt%d" % h][:, 16 * a:16 * b], T.wgs[:, 0:32].indirect(T.go[:, 8 * min(X[h]) + a:8 * min(X[h]) + b]))
-    v_gt = v(V.tensor_copy(*gate(0, 0, 16)))
+    v_gt0 = v(V.tensor_copy(*gate(0, 0, 16)))
     need("s", DWG, v_go)
     s_gt0 = s(S.activation(*gate(0, 16, 32), F.Copy))
     s_gt1 = s(S.activation(*gate(1, 8, 32), F.Copy))
-    need("v", v_gt, s_gt0)
-    v_gq = [v(V.quantize_mx(T.gq0[:, 0:128], T.gc0[:, 0:128], T.gt0[:, 0:512])), None]
     v_gt = v(V.tensor_copy(*gate(1, 0, 8)))
+    need("v", s_gt0, v_gt0)
+    v_gq = [v(V.quantize_mx(T.gq0[:, 0:128], T.gc0[:, 0:128], T.gt0[:, 0:512])), None]
 
     need("v", DX)
     v_xq = v(V.quantize_mx(T.xq[:, 0:256], T.xc[:, 0:256], T.xs[:, 0:1024]))
     plane = lambda k: (T.xp[:, 256 * k:256 * k + 256], T.xs[:, k:1024:4])
     sv, ss = [T.ps4, T.ps6], [T.ps5, T.ps7]
-    t_sv, t_ss = [None, None], [None, None]
 
     def score(h):
         need("t", v_xq, v_gq[h])
-        mm = lambda out: t(PE.matmul_mx(out, T["gq%d" % h][:, 0:128], T["gc%d" % h][:, 0:128], T.xq[:, 0:256], T.xc[:, 0:256], True, True))
-        t_sv[h] = mm(sv[h][:, 0:256])
-        t_ss[h] = mm(ss[h][:, 0:256])
+        for n, bank in (("sv", sv), ("ss", ss)):
+            D[n, h] = t(PE.matmul_mx(bank[h][:, 0:256], T["gq%d" % h][:, 0:128], T["gc%d" % h][:, 0:128], T.xq[:, 0:256], T.xc[:, 0:256], True, True))
 
-    v_own, v_es, v_e, v_rk, s_rk, s_sg = [None, None], [None, None], [None, None], [None, None], [None, None], [{}, {}]
     slot = lambda h, b: T["cs%d" % h][:, 128 * b + 127:128 * b + 128]
 
     def own(h, a, b):
-        need("v", t_sv[h])
-        v_own[h] = v(V.transpose(T["tt%d" % h][:, 32 * a:32 * b], sv[h][:, 32 * a:32 * b]))
+        need("v", ("sv", h))
+        x = v(V.transpose(T["tt%d" % h][:, 32 * a:32 * b], sv[h][:, 32 * a:32 * b]))
+        D.update({("own", h, k): x for k in range(a, b)})
 
     def equal(h):
-        need("v", v_own[h])
-        x = tt(T["eqb%d" % h][:], sv[h][:, 0:256], T["tt%d" % h][:], A.is_equal)
-        need("v", x, v_blk)
-        v_es[h] = v(V.tensor_tensor_scan(T["es%d" % h][:], T.blk[:], T["eqb%d" % h][:], 0.0, A.mult, A.subtract))
+        need("v", *[("own", h, k) for k in range(8)])
+        D["eq", h] = tt(T["eqb%d" % h][:], sv[h][:, 0:256], T["tt%d" % h][:], A.is_equal)
 
-    def compare(h):
-        P, cm = sv[h], T["cmp%d" % h]
-        need("v", v_own[h])
-        for b in range(8 - len(SB[h])):
-            m, o = 32 * (b + 1), T["tt%d" % h][:, 32 * b:32 * b + 1]
-            ts(cm[:, 256 * b:256 * b + m], P[:, 0:m], o, None, A.is_ge)
-            x = ts(cm[:, 256 * b + m:256 * b + 256], P[:, m:256], o, None, A.is_gt)
-        return x
+    def later(h):
+        need("v", ("eq", h), v_blk)
+        D["es", h] = v(V.tensor_tensor_scan(T["es%d" % h][:], T.blk[:], T["eqb%d" % h][:], 0.0, A.mult, A.subtract))
 
-    def total(h, x):
+    def compare(h, b):
+        P, cm, m, o = sv[h], T["cmp%d" % h], 32 * (b + 1), T["tt%d" % h][:, 32 * b:32 * b + 1]
+        need("v", ("own", h, b))
+        ts(cm[:, 256 * b:256 * b + m], P[:, 0:m], o, None, A.is_ge)
+        D["read", h] = D["cmp", h, b] = ts(cm[:, 256 * b + m:256 * b + 256], P[:, m:256], o, None, A.is_gt)
+
+    def total(h, *blocks):
         cm = T["cmp%d" % h]
-        need("v", x, v_es[h])
-        for b in range(8 - len(SB[h])):
-            v_rk[h] = v(V.tensor_tensor_scan(T["cs%d" % h][:, 128 * b:128 * b + 128], cm[:, 256 * b:256 * b + 128], cm[:, 256 * b + 128:256 * b + 256],
-                                             T["es%d" % h][:, 32 * b + 31:32 * b + 32], A.add, A.add))
-
-    def signs(h, blocks):
-        need("s", t_ss[h], v_own[h])
         for b in blocks:
-            s_sg[h][b] = s(S.activation(T["sg%d" % h][:, SW * b:SW * b + 256], ss[h][:, 0:256], F.Sign, bias=T["tt%d" % h][:, 32 * b:32 * b + 1], scale=-1.0))
+            need("v", ("cmp", h, b), ("es", h))
+            D["vrk", h] = v(V.tensor_tensor_scan(T["cs%d" % h][:, 128 * b:128 * b + 128], cm[:, 256 * b:256 * b + 128], cm[:, 256 * b + 128:256 * b + 256],
+                                                 T["es%d" % h][:, 32 * b + 31:32 * b + 32], A.add, A.add))
 
-    def sums(h, blocks):
-        sg, ac = T["sg%d" % h], T["ac%d" % h]
-        last = {}
-        for b in blocks:
-            need("s", s_sg[h][b], p_m)
+    def signs(h):
+        sg, ac, x = T["sg%d" % h], T["ac%d" % h], {}
+        for b in SB[h]:
+            need("s", ("ss", h), ("own", h, b))
+            x[b] = s(S.activation(sg[:, SW * b:SW * b + 256], ss[h][:, 0:256], F.Sign, bias=T["tt%d" % h][:, 32 * b:32 * b + 1], scale=-1.0))
+        for b in SB[h]:
+            need("s", x[b], p_m)
             m = SW * b + 32 * (b + 1)
             lo, hi = sg[:, SW * b:m], sg[:, m:SW * b + SW]
-            last[b] = s(S.activation(lo, lo, F.Relu, accum_out=ac[:, b:b + 1]))
+            x[b] = s(S.activation(lo, lo, F.Relu, accum_out=ac[:, b:b + 1]))
             if b < 7:
-                last[b] = s(S.activation(hi, hi, F.Relu, scale=-1.0, accum_out=ac[:, 8 + b:9 + b]))
-        for b in blocks:
-            need("s", last[b])
-            s_sg[h][b] = s(S.activation(ac[:, 16 + b:17 + b], ac[:, b:b + 1], F.Identity, scale=-1.0, bias=ac[:, 8 + b:9 + b] if b < 7 else 256.0))
+                x[b] = s(S.activation(hi, hi, F.Relu, scale=-1.0, accum_out=ac[:, 8 + b:9 + b]))
+            if b > SB[h][0]:
+                join(h, b - 1, x[b - 1])
+        join(h, b, x[b])
 
-    def settle(h, blocks):
-        for b in blocks:
-            need("s", s_sg[h][b], v_es[h])
-            s_rk[h] = s(S.activation(slot(h, b), T["ac%d" % h][:, 16 + b:17 + b], F.Identity, bias=T["es%d" % h][:, 32 * b + 31:32 * b + 32]))
+    def join(h, b, x):
+        ac = T["ac%d" % h]
+        need("s", x)
+        D["sum", h, b] = s(S.activation(ac[:, 16 + b:17 + b], ac[:, b:b + 1], F.Identity, scale=-1.0, bias=ac[:, 8 + b:9 + b] if b < 7 else 256.0))
 
-    v_of = [None, None]
-
-    def invert(h):
-        B = lambda n: T["%s%d" % (n, h)]
-        need("v", v_rk[h], s_rk[h])
-        x = v(V.tensor_copy(B("ru")[:], B("cs")[:, 127:1024:128]))
-        need("v", x, v_tok, p_wn[h])
-        x = v(V.tensor_copy(B("wn")[:, 0:256].indirect(B("ru")[:, 0:8]), T.tokv[:, 0:128]))
-        need("v", x, v_do)
-        x = v(V.tensor_copy(B("dp")[:], B("wn")[:, 0:CK].indirect(T.do[:, 0:6])))
-        need("v", x)
-        need("v", v(V.transpose(B("tw")[:], B("dp")[:])))
-        for a, e in enumerate(sorted(X[h])):
-            k = 3 * where[e][1]
-            x = tt(B("yl")[0:32, k:k + 3], B("tw")[32 * a:32 * a + 32, 0:96:32], B("tw")[32 * a:32 * a + 32, 16:96:32], A.add)
-        need("v", x)
-        for a in range(4):
-            v_of[h] = v(V.tensor_copy(B("of")[32 * a:32 * a + 32, :], B("yl")[0:32, :]))
-
-    gat = lambda h, k: (T["xg%d" % h][:, k:4 * W4:4], T.xp[:, 256 * k:256 * k + 256].indirect(T["of%d" % h][:, 0:12]))
-    s_g = [None, None]
-
-    def pick_s(h):
-        need("s", s_xp, v_xp, v_of[h])
-        for k in (0, 1):
-            s_g[h] = s(S.activation(*gat(h, k), F.Copy))
-
-    def pick_v(h):
-        need("v", s_xp, v_xp, v_of[h])
-        for k in (2, 3):
-            x = v(V.tensor_copy(*gat(h, k)))
-        return x
+    def settle(h):
+        for b in SB[h]:
+            need("s", ("sum", h, b), ("es", h))
+            D["srk", h] = s(S.activation(slot(h, b), T["ac%d" % h][:, 16 + b:17 + b], F.Identity, bias=T["es%d" % h][:, 32 * b + 31:32 * b + 32]))
 
     ls = [0]
     near_m = {"q": [near_e[0:4], near_e[4:6], near_e[6:8]], "c": [near_e[4:8], near_e[0:2], near_e[2:4]]}
     share = lambda ks, k: far_e[0::2][ks.index(k)::len(ks)]
-    masks = {"af": {z: [share(ks, k) for k in range(4) for y, ks, _ in CALLS[0] + CALLS[1] if z in y and k in ks] for z in "qc"}, "rf": {z: [far_e[2 * k:2 * k + 2] for k in range(4)] for z in "qc"},
+    masks = {"af": {z: [share(ks, k) for k in range(4) for y, ks, _ in CALLS[0] + CALLS[1] if z in y and k in ks] for z in "qc"},
+             "rf": {z: [far_e[2 * k:2 * k + 2] for k in range(4)] for z in "qc"},
              "an": {z: [near_e[0:4], near_e[4:8], far_e[1::2]] for z in "qc"}, "rn": near_m}
     mine = lambda n, d: sum(len(masks[n][z][(far_of(d) if d in far else near_of(d)).index(rank)]) for z in "qc")
     AF, AN, RN = [(n, sum(mine(n, d) for d in ds)) for n, ds in (("af", far), ("an", others), ("rn", others))]
@@ -243,15 +225,84 @@ def rank_program(g, core, T, topo):
     in_far = lambda d: CK * far_of(d).index(rank)
     in_near = lambda d: CK * near_of(d).index(rank)
 
-    def dispatch(h, x):
-        src = "tn"[h]
-        need("v", x, s_g[h])
-        x = v(V.quantize_mx(T[src + "q"][:, 0:W4], T[src + "c"][:, 0:W4], T["xg%d" % h][:, 0:4 * W4]))
-        need("p", x)
-        for z, ks, near in CALLS[h]:
-            send([(far[k], "t", CK * k, "n", 336 + in_far(far[k]), "af") for k in ks]
-                 + [(d, "n", CK * k, "n", W4 + in_near(d), "an") for k, d in enumerate(others) if near], z)
-        return x
+    def dispatch(h):
+        B = lambda n: T["%s%d" % (n, h)]
+        gat = lambda k: (B("xg")[:, k:4 * W4:4], T.xp[:, 256 * k:256 * k + 256].indirect(B("of")[:, 0:12]))
+        x = [None]
+
+        def offsets():
+            need("v", ("vrk", h), ("srk", h))
+            x[0] = v(V.tensor_copy(B("ru")[:], B("cs")[:, 127:1024:128]))
+
+        def scatter():
+            need("v", x[0], v_tok, p_wn[h])
+            x[0] = v(V.tensor_copy(B("wn")[:, 0:256].indirect(B("ru")[:, 0:8]), T.tokv[:, 0:128]))
+
+        def twice():
+            need("v", x[0], v_do)
+            x[0] = v(V.tensor_copy(B("dp")[:], B("wn")[:, 0:CK].indirect(T.do[:, 0:6])))
+
+        def turn():
+            need("v", x[0])
+            x[0] = v(V.transpose(B("tw")[:], B("dp")[:]))
+
+        def collect():
+            need("v", x[0])
+            for a, e in enumerate(sorted(X[h])):
+                k = 3 * where[e][1]
+                x[0] = tt(B("yl")[0:32, k:k + 3], B("tw")[32 * a:32 * a + 32, 0:96:32], B("tw")[32 * a:32 * a + 32, 16:96:32], A.add)
+
+        def spread():
+            need("v", x[0])
+            for a in range(4):
+                D["of", h] = v(V.tensor_copy(B("of")[32 * a:32 * a + 32, :], B("yl")[0:32, :]))
+            need("s", s_xp, v_xp, ("of", h))
+            for k in (0, 1):
+                D["sg", h] = s(S.activation(*gat(k), F.Copy))
+
+        def pick():
+            need("v", s_xp, v_xp, ("of", h))
+            for k in (2, 3):
+                x[0] = v(V.tensor_copy(*gat(k)))
+
+        def pack():
+            need("v", x[0], ("sg", h))
+            D["tile", h] = v(V.quantize_mx(T["tn"[h] + "q"][:, 0:W4], T["tn"[h] + "c"][:, 0:W4], B("xg")[:, 0:4 * W4]))
+            need("p", ("tile", h))
+            for z, ks, near in CALLS[h]:
+                send([(far[k], "t", CK * k, "n", 336 + in_far(far[k]), "af") for k in ks]
+                     + [(d, "n", CK * k, "n", W4 + in_near(d), "an") for k, d in enumerate(others) if near], z)
+
+        return [offsets, scatter, twice, turn, collect, spread, pick, pack]
+
+    def weights(i):
+        need("v", DW)
+        D["wq"] = v(V.quantize_mx(T.wq[:, 128 * i:128 * i + 128], T.wc[:, 128 * i:128 * i + 128], T.w1s[:, 512 * i:512 * i + 512]))
+
+    def unit(b):
+        need("v", p_z)
+        D["eb"] = v(V.quantize_mx(T.eq[:, 128 * b:128 * b + 128], T.ec[:, 128 * b:128 * b + 128], T.z[:, 3 - b:515 - b]))
+
+    def shifted(h):
+        need("v", ("of", h))
+        D["ol", h] = v(V.tensor_copy(T["ol%d" % h][:, 0:9], T["of%d" % h][:, 3:12]))
+
+    def chain(h):
+        steps = []
+        for e in sorted(X[h]):
+            a = where[e][1]
+            at = T["tb%d" % h][:].indirect(T["ol%d" % h][:, 3 * a - 3:3 * a] if a % 2 else T["of%d" % h][:, 3 * a:3 * a + 3])
+            out = (T.pl if 0 in X[h] else T.lk)[:, W4 * h + CK * a:W4 * h + CK * a + CK]
+
+            def look(at=at, out=out):
+                need("v", ("put", h))
+                D["look", h] = v(V.tensor_copy(out, at))
+
+            def put(at=at, e=e):
+                need("v", p_id, ("ol", h), *([("look", h)] if e % 4 else []))
+                D["put", h] = v(V.tensor_copy(at, T.idr[:, CK * e:CK * e + CK]))
+            steps += [look, put] if e % 4 else [put]
+        return steps
 
     score(0)
     need("v", s_gt1, v_gt)
@@ -262,59 +313,49 @@ def rank_program(g, core, T, topo):
     need("s", DX)
     for k in (0, 1):
         s_xp = s(S.activation(*plane(k), F.Copy))
-    own(0, 0, 8)
-    signs(0, SB[0])
-    equal(0)
-    sums(0, SB[0])
-    settle(0, SB[0])
-    need("s", p_tok, v_pf)
-    v_tok = s(S.activation(T.tokv[:], T.tok0[:], F.Identity, bias=p16))
-    x = compare(0)
-    own(1, SB[1][0], 8)
-    total(0, x)
-    signs(1, SB[1])
-    sums(1, SB[1][:1])
-    invert(0)
-    pick_s(0)
-    sums(1, SB[1][1:])
-    dispatch(0, pick_v(0))
-    own(1, 0, SB[1][0])
-    equal(1)
-    settle(1, SB[1])
-    v_read = compare(1)
-    total(1, v_read)
-    invert(1)
-    pick_s(1)
-    v_near = dispatch(1, pick_v(1))
+    do = lambda f, *a: lambda: f(*a)
+    own(0, 0, 1), own(0, 5, 8), own(0, 1, 5)
+    signs(0)
+    compare(0, 0), equal(0), compare(0, 1), later(0)
+    settle(0)
+    compare(0, 2), own(1, 3, 8), total(0, 0, 1)
+    signs(1)
+    compare(0, 3), total(0, 2), compare(0, 4), total(0, 3), own(1, 0, 3), total(0, 4)
+    first, second = dispatch(0), dispatch(1)
+    weave(first, [do(equal, 1), do(compare, 1, 0), both(do(later, 1), do(settle, 1)), do(compare, 1, 1), do(compare, 1, 2), do(total, 1, 0, 1, 2), second[0]])
+    shifted(0)
+    weave(second[1:], chain(0))
 
-    table = T.pl[:, 384:640]
+    low = where[0][0]
 
-    v_chain = []
+    def older():
+        need("v", ("put", low))
+        D["old"] = v(V.tensor_copy(T.old[:], T["tb%d" % low][:].indirect(T["of%d" % (1 - low)][:, 0:12])))
 
-    def chain(upto):
-        for e in range(len(v_chain), upto):
-            h, a = where[e]
-            at = table.indirect(T["ol%d" % h][:, 3 * a - 3:3 * a] if a % 2 else T["of%d" % h][:, 3 * a:3 * a + 3])
-            o = W4 * h + CK * a
-            if e:
-                need("v", v(V.tensor_copy(T.pl[:, o:o + CK], at)))
-            v_chain.append(v(V.tensor_copy(at, T.idr[:, CK * e:CK * e + CK])))
-            need("v", v_chain[-1])
+    def newest():
+        need("v", ("put", 0), ("put", 1))
+        D["last"] = tt(T.pl[:, 384:640], T.tb0[:], T.tb1[:], A.max)
 
-    def addresses(v_chain):
-        need("s", v_chain, v_mk)
-        dg = [T["dg%d" % k] for k in range(4)]
-        s_dg = [s(S.activation(dg[k][:], T.pl[:, k:640:4], F.Identity, scale=T.mk[:, k:k + 1])) for k in range(4)]
-        need("v", s_dg[1])
-        tt(T.d01[:], dg[0][:], dg[1][:], A.add)
-        need("v", s_dg[3])
-        need("v", tt(T.d23[:], dg[2][:], dg[3][:], A.add))
-        need("v", tt(T.dd[:], T.d01[:], T.d23[:], A.add))
-        return ts(T.op[:], T.dd[:], p3, None, A.add)
+    def merge():
+        need("v", "old", ("look", 1 - low))
+        D["earlier"] = tt(T.pl[:, W4 * (1 - low):W4 * (2 - low)], T.lk[:, W4 * (1 - low):W4 * (2 - low)], T.old[:], A.max)
+
+    def select(a, b, n, m, ready):
+        need("s", ready, v_mk)
+        for k in range(n):
+            D["sel", a] = s(S.activation(T.dg[:, a + k:b:n], T.pl[:, a + k:b:n], F.Identity, scale=T.mk[:, m + k:m + k + 1]))
+
+    def gather_up(a, b):
+        need("v", ("sel", a))
+        D["up", a] = v(V.tensor_tensor_scan(T.dd[:, a:b], T.keep[:, a:b], T.dg[:, a:b], 0.0, A.mult, A.add))
+
+    def address(a, b, n, c, o):
+        need("v", ("up", a))
+        D["op", a] = ts(T.op[:, o:o + (b - a) // n], T.dd[:, a + n - 1:b:n], c, None, A.add)
 
     def expert(h, ready):
         a, banks, hh = (336, 144)[h], [4 * h + i for i in range(4)], T["hh%d" % h]
-        need("t", v_wq, *ready)
+        need("t", "wq", *ready)
         tm = [t(PE.matmul_mx(T["ps%d" % k][:, 0:W4], T.wq[:, 128 * i:128 * i + 128], T.wc[:, 128 * i:128 * i + 128],
                              T.nq[:, a:a + W4], T["nc"][:, a:a + W4], True, True)) for i, k in enumerate(banks)]
         for i in (0, 2):
@@ -331,35 +372,40 @@ def rank_program(g, core, T, topo):
             send(back[h] + (back[1] if HOLD[rank] else []))
         return [s_r, v_r, x]
 
-    need("v", DW)
-    v_wq = v(V.quantize_mx(T.wq[:, 0:512], T.wc[:, 0:512], T.w1s[:, 0:2048]))
-    for h in range(2):
-        x = v(V.tensor_copy(T["ol%d" % h][:, 0:9], T["of%d" % h][:, 3:12]))
-    need("v", x, p_id)
     free = [None, None]
-    arrived = [[AF], [AN, v_near, v_read, s_rk[1]]]
+    arrived = [[AF], [AN, ("tile", 1), ("read", 1), ("srk", 1)]]
     place = sorted(X[1]).index(rank)
+    shifted(1)
+    weights(0), weights(1)
+    links, rest = chain(1), [do(weights, 2), do(weights, 3)] + [do(unit, b) for b in range(4)]
     for step in STEPS[place]:
         if step in ("f", "n"):
             free["fn".index(step)] = expert("fn".index(step), arrived["fn".index(step)])
+        elif step == "m":
+            older(), newest(), merge()
+        elif step == "s":
+            select(0, 384, 8, 0, "earlier")
+            select(384, 640, 4, 8, "last")
+        elif step == "a":
+            gather_up(0, 384), gather_up(384, 640), address(0, 384, 8, p1, 0), address(384, 640, 4, pc, 48)
         else:
-            chain(step)
-    v_op = addresses(v_chain[-1])
+            weave(links[:step], rest)
+            links = links[step:]
 
     banks = [free[0] + free[1], free[0] + free[1]]
-    turn = [0]
+    turns = [0]
 
     def unpack(a, n, arrived):
-        k = turn[0] % 2
-        turn[0] += 1
-        need("t", v_eb, arrived, *banks[k])
+        k = turns[0] % 2
+        turns[0] += 1
+        need("t", "eb", arrived, *banks[k])
         return k, [t(PE.matmul_mx(T["ps%d" % (4 * k + b)][:, 0:n], T.eq[:, 128 * b:128 * b + 128], T.ec[:, 128 * b:128 * b + 128],
                                   T.mq[:, a:a + n], T.mc[:, a:a + n], True, True)) for b in range(4)]
 
     def fetch(q, u, b, e, c, n, *ready):
         h, a = where[e]
-        buf, at = (T.pb, 16) if e == 0 else (T["ds%d" % h], W4 * a)
-        o, i = buf[:, at + b:at + W4 * n:4], T["ps%d" % (4 * u[0] + b)][:, c:c + CK * n]
+        buf, at = (T.pb, HALF * (b // 2) + 8) if e == 0 else (T["ds%d" % h], 4 * W2 * (b // 2) + W2 * a)
+        o, i = buf[:, at + b % 2:at + W2 * n:2], T["ps%d" % (4 * u[0] + b)][:, c:c + CK * n]
         need(q, u[1][b], *ready)
         return s(S.activation(o, i, F.Copy)) if q == "s" else v(V.tensor_copy(o, i))
 
@@ -368,12 +414,14 @@ def rank_program(g, core, T, topo):
     def add(upto):
         for e in range(added[0] + 1, upto + 1):
             h, a = where[e]
-            need("v", v_op, *(ready.get(e, []) + ready[0]))
-            o, k = 16 + W4 * e, 48 * h + 12 * a
-            x = tt(T.pb[:, o:o + W4], T.pb[:, 0:o].indirect(T.op[:, k:k + 12]), T["ds%d" % h][:, W4 * a:W4 * a + W4], A.add)
-            need("v", x)
+            need("v", ("op", 0), *(ready.get(e, []) + ready[0]))
+            o, k = 8 + W2 * e, 24 * h + 6 * a
+            for c in range(2):
+                need("v", *([("add", c)] if e > 1 else []))
+                d = 4 * W2 * c + W2 * a
+                D["add", c] = tt(T.pb[:, HALF * c + o:HALF * c + o + W2], T.pb[:, HALF * c:HALF * c + o].indirect(T.op[:, k:k + 6]),
+                                 T["ds%d" % h][:, d:d + W2], A.add)
             added[0] = e
-        return x
 
     def far_in(k, queues):
         u = unpack(528 + CK * (k + 1) - 128, 128, RF[k])
@@ -387,19 +435,19 @@ def rank_program(g, core, T, topo):
         add(2)
     else:
         u = unpack(0, W4, RN)
-        first = [fetch("sv"[b % 2], u, b, e, CK * where[e][1], 1) for b in range(4) for e in (0, 1)]
-        ready[0] = first[-3:]
+        one = [fetch("sv"[b % 2], u, b, e, CK * where[e][1], 1) for b in range(4) for e in (0, 1)]
+        ready[0] = one[-3:]
         pair = min((2, 3), key=lambda e: where[e][1])
-        banks[u[0]] = ready[2] = [fetch("s", u, b, pair, CK * where[pair][1], 2, *first[-1:] * (b % 2)) for b in (0, 2, 1, 3)][-1:]
+        banks[u[0]] = ready[2] = [fetch("s", u, b, pair, CK * where[pair][1], 2, *one[-1:] * (b % 2)) for b in (0, 2, 1, 3)][-1:]
         for k in range(3):
             far_in(k, "ss")
         add(6)
     far_in(3, "sv")
-    x = add(7)
-    win = T.pb[:, 0:16 + N * W4]
-    need("s", x)
+    add(7)
+    need("v", ("add", 1), ("op", 384))
+    need("s", ("add", 1), ("op", 384))
     for a in (0, 512):
-        part = lambda c: (T.yt[:, c:c + 256], win.indirect(T.op[:, 96 + c // 16:112 + c // 16]))
+        part = lambda c: (T.yt[:, c:c + 256], T.pb[:].indirect(T.op[:, 48 + c // 16:64 + c // 16]))
         need("y", v(V.tensor_copy(*part(a))), s(S.activation(*part(a + 256), F.Copy)))
         g.sync.dma_start(T.y[:, a:a + 512], T.yt[:, a:a + 512]).then_inc(T.sem.dy, 16)
 

@@ -3,14 +3,27 @@ from concourse.mybir import dt, AluOpType as A, ActivationFunctionType as F
 
 CK = 48
 W4 = 4 * CK
-SB = [[5, 6, 7], [3, 4, 5, 6, 7]]
+SB = [[5, 6, 7], [4, 5, 6, 7]]
 SW = 257
 W2 = 2 * CK
 HALF = 8 + 8 * W2
 
-CALLS = [[("q", [0], False), ("c", [0, 1], False), ("q", [1], False)], [("q", [2], True), ("c", [2, 3], True), ("q", [3], False)]]
-STEPS = [(5, "f", 2, "n", "m", "s", "a"), (7, "f", "n", "m", "s", "a"), (7, "m", "n", "f", "s", "a"), (7, "m", "n", "f", "s", "a")]
-HOLD = [e in (2, 6, 7) for e in range(8)]
+FIRST = [[4, 5, 6, 7], [0, 1, 2, 3]]
+EVEN, ODD, LOW, HIGH = [0, 2, 4, 6], [1, 3, 5, 7], [8, 9, 10, 11], [12, 13, 14, 15]
+PAIRS = [[0, 1], [2, 3], [4, 5], [6, 7]]
+CALLS = [[[("q", [4, 7], [EVEN, LOW]), ("c", [4, 5, 6, 7], [ODD[:2], ODD[2:3], ODD[3:], LOW]), ("q", [5], [EVEN]), ("q", [6], [EVEN])],
+          [("q", [0, 1, 2, 3], [LOW, HIGH, ODD]), ("c", [0, 1, 2, 3], [LOW, HIGH, EVEN])]],
+         [[("q", [0], [EVEN]), ("c", [0, 1, 2, 3], [[k] for k in ODD]), ("q", [1], [EVEN]), ("q", [2], [EVEN])],
+          [("q", [3, 4, 5, 6, 7], [EVEN, LOW, HIGH, ODD]), ("c", [4, 5, 6, 7], [LOW, HIGH, EVEN])]]]
+ROUND = 7
+AT = [[0, 3, 6, 9], [0, 3, 6, 9]]
+UNITS = [[([0, 1, 2, 3], True), ([4], False), ([5], False), ([6], False), ([7], True)],
+         [([0], False), ([1], False), ([2], False), ([4, 5, 6, 7], False), ([3], True)]]
+END = [0, 2]
+STEPS = [(2, "f", 2, "n", 1), (3, "f", 1, "n", 1), (4, "f", "n", 1), (5, "n", "f")] * 2
+
+ENG = {"rf": {z: PAIRS for z in "qc"},
+       "rn": {"q": [LOW, HIGH[:2], HIGH[2:]], "c": [HIGH, LOW[:2], LOW[2:]]}}
 
 SCRATCH = {}
 
@@ -23,29 +36,58 @@ def _sbuf(dtype, names):
 
 
 _sbuf("bfloat16", "wgs:32 xs:1024 xp:1024 w1s:2048 ones:128 z:516 col:256 blk:256 tok0:128 tokv:128 hh@:768 gt@:512 cmp@:2048 cs@:1024 sg@:%d "
-      "eqb@:256 es@:256 wn@:256 dp@:96 tw@:96 yl@:12 xg@:768" % (8 * SW))
+      "eqb@:256 es@:256 wn@:256 dp@:96 tw@:96 yl@:14 xg@:768" % (8 * SW))
 for _d, _s in (("float8_e4m3fn_x4", "q"), ("uint8", "c")):
     _sbuf(_d, " ".join("%s%s%s" % (w[0], _s, w[1:]) for w in "x:256 w:512 e:512 t:192 n:528 m:720 g@:128".split()))
 _sbuf("int32", "ic:1 pi:8")
-_sbuf("float32", "e4:64 pf:9 do0:6 mk:12 idr:384 pl:640 lk:384 old:192 tb@:256 dg:640 keep:640 dd:640")
+_sbuf("float32", "e4:64 pf:9 do0:6 mk:12 idr:384 pl:384 old:384 tb@:256 tl:256 dg:640 keep:448 dd:640")
 _sbuf("float32", "ds@:768 pb:%d yt:1024 tt@:256 ac@:24" % (2 * HALF))
-_sbuf("uint16", "go:64 do:6 op:112 ru@:8 ol@:10 of@:12")
+_sbuf("uint16", "go:64 do:6 op:112 ru@:8 ol@:14 of@:14")
 for _b in range(8):
     SCRATCH["ps%d" % _b] = ("psum", [128, 512], "float32")
 
-SEMAPHORES = ["v", "t", "s", "p", "dwg", "dx", "dw", "af", "an", "rf0", "rf1", "rf2", "rf3", "rn", "ls", "dy"]
+SEMAPHORES = ["v", "t", "s", "p", "dwg", "dx", "dw", "af", "an", "ls", "dy"] + ["r%d" % e for e in range(8)]
+
+
+def runs(items, follows):
+    out = []
+    for e in items:
+        if out and follows(out[-1][-1], e):
+            out[-1].append(e)
+        else:
+            out.append([e])
+    return out
 
 
 def rank_program(g, core, T, topo):
     rank = T.rank_of(core)
-    if rank is None:
-        return
     N = len(T.cores)
     near_of = lambda r: [k for k in range(N) if k != r and topo.chip(T.cores[k]) == topo.chip(T.cores[r])]
     far_of = lambda r: [k for k in range(N) if topo.chip(T.cores[k]) != topo.chip(T.cores[r])]
+    helper = {r: [c for c in topo.cores_of(T.cores[r]) if topo.die(c) != topo.die(T.cores[r])][k] for k, r in enumerate(far_of(ROUND))}
+
+    def transfer(z, to, src, a, dst, b, sem, eng):
+        rid, pid, _ = topo.addr(to)
+        sa, da = T[src + z][:, a:a + CK], T[dst + z][:, b:b + CK]
+        if z == "q":
+            sa, da = sa.bitcast(dt.uint8), da.bitcast(dt.uint8)
+        return RemoteDMATransfer(dst_ids=[DstId(rid=rid, pnc=pid)], dma_engine_mask=sum(1 << e for e in eng), remote_sem=T.sem[sem], src=sa, dst=da)
+
+    if rank is None:
+        for k, r in enumerate(far_of(ROUND)):
+            if helper[r] == core:
+                eng = topo.engines(core, T.cores[ROUND])
+                g.wait_ge(T.sem.af, 2 * len(LOW))
+                for z, places in (("q", EVEN), ("c", EVEN)):
+                    g.remote_dma_fused([transfer(z, T.cores[ROUND], "t", 0, "n", 336 + CK * k, "af", [eng[i] for i in places])], local_sem=T.sem.ls)
+                g.wait_ge(T.sem.ls, 2 * len(EVEN))
+        return
     others, far = near_of(rank), far_of(rank)
-    X = [far, others + [rank]]
+    side = lambda r: int(0 in far_of(r))
+    X = [sorted((e for e in range(N) if (e in FIRST[side(rank)]) != h), key=lambda e: (e == rank, e)) for h in range(2)]
     where = {e: (h, a) for h in range(2) for a, e in enumerate(X[h])}
+    back = others[::-1] + [rank]
+    lies = {e: (c, a) for c, es in enumerate((far, back)) for a, e in enumerate(es)}
     far_e = topo.engines(core, T.cores[far[0]])
     near_e = [e for e in topo.engines(core, T.cores[others[0]]) if e not in far_e]
 
@@ -87,6 +129,9 @@ def rank_program(g, core, T, topo):
 
     imp = dict(allow_small_or_imprecise_dtypes=True)
     p_ic = p(g.iota(T.ic[:], [[0, 1]], 0, 1))
+    v(V.memset(T.ones[:], 1.0))
+    need("p", v(V.memset(T.z[:], 0.0)))
+    p_z = p(g.affine_select(T.z[:, 3:515:4], T.ones[:], [[-1, 128]], A.is_equal, 0.0, 0, 1))
     p_e4 = p(g.iota(T.e4[:], [[4, N], [0, 8]], 0, 0, **imp))
     p_do = p(g.iota(T.do0[:], [[16, 3], [0, 2]], 0, 0, **imp))
     p_col = p(g.iota(T.col[:], [[0, 8], [1, 32]], 0, 0, **imp))
@@ -95,37 +140,39 @@ def rank_program(g, core, T, topo):
         p_m = p(g.iota(T["sg%d" % h][:, SW - 1:8 * SW:SW], [[-32, 8]], -32, 0, **imp))
     fill = lambda ap, n, c=0: p(g.iota(ap, [[0, n]], c, 0, **imp))
     p_wn = [fill(T["wn%d" % h][:, 0:CK], CK) for h in range(2)]
-    v(V.memset(T.ones[:], 1.0))
-    need("p", v(V.memset(T.z[:], 0.0)))
-    p_z = p(g.affine_select(T.z[:, 3:515:4], T.ones[:], [[-1, 128]], A.is_equal, 0.0, 0, 1))
-    need("p", fill(T.keep[:], 640, 1))
-    fill(T.keep[:, 0:384:8], 48)
-    fill(T.keep[:, 384:640:4], 64)
-    for e, buf in ((0, T.pl), (4, T.lk)):
-        fill(T["tb%d" % where[e][0]][:], 256)
-        fill(buf[:, W4 * where[e][0] + CK * where[e][1]:W4 * where[e][0] + CK * where[e][1] + CK], CK)
-    for a in (0, HALF):
-        fill(T.pb[:, a:a + 8], 8)
+    need("p", fill(T.keep[:], 448, 1))
+    fill(T.keep[:, 0:192:8], 24)
+    fill(T.keep[:, 192:448:4], 64)
+    for h in range(2):
+        fill(T["tb%d" % h][:], 256)
     p_id = p(g.iota(T.idr[:], [[W2, N], [2, CK]], 8, 0, **imp))
+
+    def unit(b):
+        need("v", p_z)
+        D["eb"] = v(V.quantize_mx(T.eq[:, 128 * b:128 * b + 128], T.ec[:, 128 * b:128 * b + 128], T.z[:, 3 - b:515 - b]))
 
     need("v", p_ic)
     for k, m in enumerate((3, 31, 16, 15, 12, 14, 1, 2)):
         x = ts(T.pi[:, k:k + 1], T.ic[:], m, None, A.bitwise_and)
+    unit(0)
     need("v", x)
     v_pf = v(V.tensor_copy(T.pf[:, 0:8], T.pi[:]))
+    unit(1)
     p3, p31, p16, p15, p12, p14, p1, p2, pc = [T.pf[:, k:k + 1] for k in range(9)]
     need("v", v_pf, p_e4, p_do)
-    v_go = ts(T.go[:], T.e4[:], p3, None, A.add)
+    order = sorted(X[0]) + sorted(X[1])
+    for run in runs(order, lambda e, f: f == e + 1):
+        k = order.index(run[0])
+        v_go = ts(T.go[:, 8 * k:8 * (k + len(run))], T.e4[:, 8 * run[0]:8 * (run[0] + len(run))], p3, None, A.add)
     v_do = ts(T.do[:], T.do0[:], p15, None, A.add)
-    ts(pc, p2, HALF / 2, p1, A.mult, A.add)
-    need("v", p_col)
-    ts(T.mk[:, 0:8], T.col[:, 0:16:2], p14, None, A.is_equal)
-    v_mk = ts(T.mk[:, 8:12], T.col[:, 0:16:4], p12, None, A.is_equal)
-    v_blk = ts(T.blk[:], T.col[:], p31, None, A.not_equal)
-    need("s", p_tok, v_pf)
-    v_tok = s(S.activation(T.tokv[:], T.tok0[:], F.Identity, bias=p16))
+    unit(2), unit(3)
+    zero = lambda ap: lambda: v(V.memset(ap, 0.0))
+    slots = lambda buf, e, n=1: buf[:, W4 * where[e][0] + CK * where[e][1]:W4 * where[e][0] + CK * (where[e][1] + n)]
+    small = [zero(slots(T.pl, 0)), zero(slots(T.pl, 4)), zero(T.pb[:, 0:8]), zero(T.pb[:, HALF:HALF + 8]),
+             lambda: ts(pc, p2, HALF / 2, p1, A.mult, A.add), lambda: ts(T.mk[:, 0:8], T.col[:, 0:16:2], p14, None, A.is_equal),
+             lambda: ts(T.mk[:, 8:12], T.col[:, 0:16:4], p12, None, A.is_equal)]
     need("v", DWG, v_go)
-    gate = lambda h, a, b: (T["gt%d" % h][:, 16 * a:16 * b], T.wgs[:, 0:32].indirect(T.go[:, 8 * min(X[h]) + a:8 * min(X[h]) + b]))
+    gate = lambda h, a, b: (T["gt%d" % h][:, 16 * a:16 * b], T.wgs[:, 0:32].indirect(T.go[:, 32 * h + a:32 * h + b]))
     v_gt0 = v(V.tensor_copy(*gate(0, 0, 16)))
     need("s", DWG, v_go)
     s_gt0 = s(S.activation(*gate(0, 16, 32), F.Copy))
@@ -159,11 +206,13 @@ def rank_program(g, core, T, topo):
         need("v", ("eq", h), v_blk)
         D["es", h] = v(V.tensor_tensor_scan(T["es%d" % h][:], T.blk[:], T["eqb%d" % h][:], 0.0, A.mult, A.subtract))
 
-    def compare(h, b):
+    def compare(h, b, parts="ab"):
         P, cm, m, o = sv[h], T["cmp%d" % h], 32 * (b + 1), T["tt%d" % h][:, 32 * b:32 * b + 1]
         need("v", ("own", h, b))
-        ts(cm[:, 256 * b:256 * b + m], P[:, 0:m], o, None, A.is_ge)
-        D["read", h] = D["cmp", h, b] = ts(cm[:, 256 * b + m:256 * b + 256], P[:, m:256], o, None, A.is_gt)
+        if "a" in parts:
+            ts(cm[:, 256 * b:256 * b + m], P[:, 0:m], o, None, A.is_ge)
+        if "b" in parts:
+            D["read", h] = D["cmp", h, b] = ts(cm[:, 256 * b + m:256 * b + 256], P[:, m:256], o, None, A.is_gt)
 
     def total(h, *blocks):
         cm = T["cmp%d" % h]
@@ -173,25 +222,22 @@ def rank_program(g, core, T, topo):
                                                  T["es%d" % h][:, 32 * b + 31:32 * b + 32], A.add, A.add))
 
     def signs(h):
-        sg, ac, x = T["sg%d" % h], T["ac%d" % h], {}
         for b in SB[h]:
             need("s", ("ss", h), ("own", h, b))
-            x[b] = s(S.activation(sg[:, SW * b:SW * b + 256], ss[h][:, 0:256], F.Sign, bias=T["tt%d" % h][:, 32 * b:32 * b + 1], scale=-1.0))
-        for b in SB[h]:
-            need("s", x[b], p_m)
+            D["sign", h, b] = s(S.activation(T["sg%d" % h][:, SW * b:SW * b + 256], ss[h][:, 0:256], F.Sign, bias=T["tt%d" % h][:, 32 * b:32 * b + 1], scale=-1.0))
+
+    def sums(h, blocks):
+        sg, ac = T["sg%d" % h], T["ac%d" % h]
+        for b in blocks:
+            need("s", ("sign", h, b), p_m)
             m = SW * b + 32 * (b + 1)
             lo, hi = sg[:, SW * b:m], sg[:, m:SW * b + SW]
-            x[b] = s(S.activation(lo, lo, F.Relu, accum_out=ac[:, b:b + 1]))
+            D["part", h, b] = s(S.activation(lo, lo, F.Relu, accum_out=ac[:, b:b + 1]))
             if b < 7:
-                x[b] = s(S.activation(hi, hi, F.Relu, scale=-1.0, accum_out=ac[:, 8 + b:9 + b]))
-            if b > SB[h][0]:
-                join(h, b - 1, x[b - 1])
-        join(h, b, x[b])
-
-    def join(h, b, x):
-        ac = T["ac%d" % h]
-        need("s", x)
-        D["sum", h, b] = s(S.activation(ac[:, 16 + b:17 + b], ac[:, b:b + 1], F.Identity, scale=-1.0, bias=ac[:, 8 + b:9 + b] if b < 7 else 256.0))
+                D["part", h, b] = s(S.activation(hi, hi, F.Relu, scale=-1.0, accum_out=ac[:, 8 + b:9 + b]))
+            for k in range(max(b - 1, SB[h][0]), b + (b == 7)):
+                need("s", ("part", h, k))
+                D["sum", h, k] = s(S.activation(ac[:, 16 + k:17 + k], ac[:, k:k + 1], F.Identity, scale=-1.0, bias=ac[:, 8 + k:9 + k] if k < 7 else 256.0))
 
     def settle(h):
         for b in SB[h]:
@@ -199,35 +245,28 @@ def rank_program(g, core, T, topo):
             D["srk", h] = s(S.activation(slot(h, b), T["ac%d" % h][:, 16 + b:17 + b], F.Identity, bias=T["es%d" % h][:, 32 * b + 31:32 * b + 32]))
 
     ls = [0]
-    near_m = {"q": [near_e[0:4], near_e[4:6], near_e[6:8]], "c": [near_e[4:8], near_e[0:2], near_e[2:4]]}
-    share = lambda ks, k: far_e[0::2][ks.index(k)::len(ks)]
-    masks = {"af": {z: [share(ks, k) for k in range(4) for y, ks, _ in CALLS[0] + CALLS[1] if z in y and k in ks] for z in "qc"},
-             "rf": {z: [far_e[2 * k:2 * k + 2] for k in range(4)] for z in "qc"},
-             "an": {z: [near_e[0:4], near_e[4:8], far_e[1::2]] for z in "qc"}, "rn": near_m}
-    mine = lambda n, d: sum(len(masks[n][z][(far_of(d) if d in far else near_of(d)).index(rank)]) for z in "qc")
-    AF, AN, RN = [(n, sum(mine(n, d) for d in ds)) for n, ds in (("af", far), ("an", others), ("rn", others))]
-    RF = [("rf%d" % k, mine("rf", d)) for k, d in enumerate(far)]
+    pick_e = lambda sets: [[(far_e + near_e)[k] for k in ks] for ks in sets]
+    near_m, far_m = [{z: pick_e(ENG[n][z]) for z in "qc"} for n in ("rn", "rf")]
+    out = [{(z, d): eng for z, ds, sets in CALLS[side(r)][0] + CALLS[side(r)][1] for d, eng in zip([d for d in ds if d != r], pick_e(sets))}
+           for r in range(N)]
+    AF, AN = [(n, sum(len(out[r][z, rank]) for r in rs for z in "qc")) for n, rs in (("af", far), ("an", others))]
+    RB = {e: ("r%d" % e, sum(len(far_m[z][far_of(e).index(rank)] if e in far else near_m[z][near_of(e).index(rank)]) for z in "qc")) for e in far + others}
 
-    def send(parts, kinds="qc"):
-        for z in kinds:
-            tr = []
-            for d, src, a, dst, b, sem in parts:
-                rid, pid, _ = topo.addr(T.cores[d])
-                eng = masks[sem[:2]][z][(far if d in far else others).index(d)]
-                sa, da = T[src + z][:, a:a + CK], T[dst + z][:, b:b + CK]
-                if z == "q":
-                    sa, da = sa.bitcast(dt.uint8), da.bitcast(dt.uint8)
-                tr.append(RemoteDMATransfer(dst_ids=[DstId(rid=rid, pnc=pid)], dma_engine_mask=sum(1 << e for e in eng),
-                                            remote_sem=T.sem[sem], src=sa, dst=da))
-                ls[0] += len(eng)
-            g.remote_dma_fused(tr, local_sem=T.sem.ls)
+    def send(z, parts):
+        tr = []
+        for d, src, a, dst, b, sem, eng in parts:
+            if (d, sem) == (ROUND, "af"):
+                tr.append(transfer(z, helper[rank], src, a, "t", 0, sem, eng))
+            else:
+                tr.append(transfer(z, T.cores[d], src, a, dst, b, sem, eng))
+            ls[0] += len(eng)
+        g.remote_dma_fused(tr, local_sem=T.sem.ls)
 
     in_far = lambda d: CK * far_of(d).index(rank)
     in_near = lambda d: CK * near_of(d).index(rank)
 
     def dispatch(h):
         B = lambda n: T["%s%d" % (n, h)]
-        gat = lambda k: (B("xg")[:, k:4 * W4:4], T.xp[:, 256 * k:256 * k + 256].indirect(B("of")[:, 0:12]))
         x = [None]
 
         def offsets():
@@ -246,112 +285,125 @@ def rank_program(g, core, T, topo):
             need("v", x[0])
             x[0] = v(V.transpose(B("tw")[:], B("dp")[:]))
 
-        def collect():
+        def collect(a, b):
             need("v", x[0])
-            for a, e in enumerate(sorted(X[h])):
-                k = 3 * where[e][1]
-                x[0] = tt(B("yl")[0:32, k:k + 3], B("tw")[32 * a:32 * a + 32, 0:96:32], B("tw")[32 * a:32 * a + 32, 16:96:32], A.add)
+            for e in X[h][a:b]:
+                k, c = AT[h][where[e][1]], 32 * sorted(X[h]).index(e)
+                D["yl", h, a] = tt(B("yl")[0:32, k:k + 3], B("tw")[c:c + 32, 0:96:32], B("tw")[c:c + 32, 16:96:32], A.add)
 
-        def spread():
-            need("v", x[0])
-            for a in range(4):
-                D["of", h] = v(V.tensor_copy(B("of")[32 * a:32 * a + 32, :], B("yl")[0:32, :]))
-            need("s", s_xp, v_xp, ("of", h))
-            for k in (0, 1):
-                D["sg", h] = s(S.activation(*gat(k), F.Copy))
+        def spread(a, b):
+            need("v", ("yl", h, a))
+            k = AT[h][a]
+            for c in range(0, 128, 32):
+                D["of", h] = D["of", h, a] = v(V.tensor_copy(B("of")[c:c + 32, k:k + 3 * (b - a)], B("yl")[0:32, k:k + 3 * (b - a)]))
 
-        def pick():
-            need("v", s_xp, v_xp, ("of", h))
-            for k in (2, 3):
-                x[0] = v(V.tensor_copy(*gat(k)))
+        def pick(q, a, b):
+            need(q, s_xp, v_xp, ("of", h, a), *([("tile", h)] if a else []))
+            for k in (0, 1) if q == "s" else (2, 3):
+                o, i = B("xg")[:, 4 * CK * a + k:4 * CK * b:4], T.xp[:, 256 * k:256 * k + 256].indirect(B("of")[:, AT[h][a]:AT[h][a] + 3 * (b - a)])
+                D["xg", q] = s(S.activation(o, i, F.Copy)) if q == "s" else v(V.tensor_copy(o, i))
 
-        def pack():
-            need("v", x[0], ("sg", h))
-            D["tile", h] = v(V.quantize_mx(T["tn"[h] + "q"][:, 0:W4], T["tn"[h] + "c"][:, 0:W4], B("xg")[:, 0:4 * W4]))
+        def pack(a, b):
+            need("v", ("xg", "v"), ("xg", "s"))
+            src, n = ["n" if rank in es else "t" for es in X], max(128, CK * b)
+            D["tile", h] = v(V.quantize_mx(T[src[h] + "q"][:, CK * a:n], T[src[h] + "c"][:, CK * a:n], B("xg")[:, 4 * CK * a:4 * n]))
             need("p", ("tile", h))
-            for z, ks, near in CALLS[h]:
-                send([(far[k], "t", CK * k, "n", 336 + in_far(far[k]), "af") for k in ks]
-                     + [(d, "n", CK * k, "n", W4 + in_near(d), "an") for k, d in enumerate(others) if near], z)
+            calls = CALLS[side(rank)][h]
+            for z, ds, _ in calls[:1] if b < 4 else calls[a:]:
+                send(z, [(d, src[where[d][0]], CK * where[d][1], "n", 336 + in_far(d) if d in far else W4 + in_near(d), "af" if d in far else "an", out[rank][z, d])
+                         for d in ds if d != rank])
 
-        return [offsets, scatter, twice, turn, collect, spread, pick, pack]
+        return [offsets, scatter, twice, turn], collect, spread, pick, pack
 
     def weights(i):
         need("v", DW)
         D["wq"] = v(V.quantize_mx(T.wq[:, 128 * i:128 * i + 128], T.wc[:, 128 * i:128 * i + 128], T.w1s[:, 512 * i:512 * i + 512]))
 
-    def unit(b):
-        need("v", p_z)
-        D["eb"] = v(V.quantize_mx(T.eq[:, 128 * b:128 * b + 128], T.ec[:, 128 * b:128 * b + 128], T.z[:, 3 - b:515 - b]))
-
     def shifted(h):
         need("v", ("of", h))
-        D["ol", h] = v(V.tensor_copy(T["ol%d" % h][:, 0:9], T["of%d" % h][:, 3:12]))
+        D["ol", h] = v(V.tensor_copy(T["ol%d" % h][:, AT[h][1] + 1:AT[h][3] + 4], T["of%d" % h][:, AT[h][1]:AT[h][3] + 3]))
 
-    def chain(h):
+    def listed(e, n=1):
+        h, k = where[e][0], AT[where[e][0]][where[e][1]]
+        return T["ol%d" % h][:, k + 1:k + 1 + 3 * n] if k % 2 else T["of%d" % h][:, k:k + 3 * n]
+
+    def chain(c):
         steps = []
-        for e in sorted(X[h]):
-            a = where[e][1]
-            at = T["tb%d" % h][:].indirect(T["ol%d" % h][:, 3 * a - 3:3 * a] if a % 2 else T["of%d" % h][:, 3 * a:3 * a + 3])
-            out = (T.pl if 0 in X[h] else T.lk)[:, W4 * h + CK * a:W4 * h + CK * a + CK]
+        for e in range(4 * c, 4 * c + 4):
+            def look(e=e):
+                need("v", ("put", c), ("ol", where[e][0]))
+                D["look", c] = v(V.tensor_copy(slots(T.pl, e), T["tb%d" % c][:].indirect(listed(e))))
 
-            def look(at=at, out=out):
-                need("v", ("put", h))
-                D["look", h] = v(V.tensor_copy(out, at))
-
-            def put(at=at, e=e):
-                need("v", p_id, ("ol", h), *([("look", h)] if e % 4 else []))
-                D["put", h] = v(V.tensor_copy(at, T.idr[:, CK * e:CK * e + CK]))
+            def put(e=e):
+                need("v", p_id, ("ol", where[e][0]), *([("look", c)] if e % 4 else []))
+                D["put", c] = v(V.tensor_copy(T["tb%d" % c][:].indirect(listed(e)), T.idr[:, CK * e:CK * e + CK]))
             steps += [look, put] if e % 4 else [put]
         return steps
 
     score(0)
+    for k in (2, 3):
+        v_xp = v(V.tensor_copy(*plane(k)))
+    need("v", p_col, p_tok)
+    v_blk = ts(T.blk[:], T.col[:], p31, None, A.not_equal)
     need("v", s_gt1, v_gt)
     v_gq[1] = v(V.quantize_mx(T.gq1[:, 0:128], T.gc1[:, 0:128], T.gt1[:, 0:512]))
     score(1)
-    for k in (2, 3):
-        v_xp = v(V.tensor_copy(*plane(k)))
+    v_tok = ts(T.tokv[:], T.tok0[:], p16, None, A.add)
     need("s", DX)
     for k in (0, 1):
         s_xp = s(S.activation(*plane(k), F.Copy))
     do = lambda f, *a: lambda: f(*a)
-    own(0, 0, 1), own(0, 5, 8), own(0, 1, 5)
-    signs(0)
+    own(0, 5, 8), own(0, 0, 1), own(0, 1, 5)
+    signs(0), sums(0, SB[0])
     compare(0, 0), equal(0), compare(0, 1), later(0)
     settle(0)
-    compare(0, 2), own(1, 3, 8), total(0, 0, 1)
-    signs(1)
-    compare(0, 3), total(0, 2), compare(0, 4), total(0, 3), own(1, 0, 3), total(0, 4)
-    first, second = dispatch(0), dispatch(1)
-    weave(first, [do(equal, 1), do(compare, 1, 0), both(do(later, 1), do(settle, 1)), do(compare, 1, 1), do(compare, 1, 2), do(total, 1, 0, 1, 2), second[0]])
-    shifted(0)
-    weave(second[1:], chain(0))
+    compare(0, 2), own(1, 4, 8)
+    signs(1), sums(1, SB[1])
+    compare(0, 3), compare(0, 4), own(1, 0, 4), total(0, 0, 1, 2, 3, 4), equal(1)
+    steps = lambda lists, collect, spread, pick, pack: lists + [do(collect, 0, 4), both(do(spread, 0, 4), do(pick, "s", 0, 4)), do(pick, "v", 0, 4), do(pack, 0, 4)]
+    weave(steps(*dispatch(0)), [both(do(compare, 1, 0, "a"), do(compare, 1, 1, "a")), both(do(later, 1), do(settle, 1)), do(compare, 1, 0, "b"), do(compare, 1, 1, "b"),
+                                do(compare, 1, 2), do(compare, 1, 3, "a"), both(do(compare, 1, 3, "b"), do(total, 1, 0, 1, 2))])
+    total(1, 3), shifted(0), small.pop()()
+    weave(steps(*dispatch(1)), [both(*small[0:2]), do(weights, 0), both(*small[2:4]), do(weights, 1), do(weights, 2), both(*small[4:6]), do(weights, 3)])
+    links, rest = chain(where[0][0]), chain(where[4][0])
+    shifted(1)
 
-    low = where[0][0]
+    high = [run for h in range(2) for run in runs([e for e in X[h] if e >= 4], lambda e, f: AT[h][where[f][1]] == AT[h][where[e][1]] + 3)]
 
     def older():
-        need("v", ("put", low))
-        D["old"] = v(V.tensor_copy(T.old[:], T["tb%d" % low][:].indirect(T["of%d" % (1 - low)][:, 0:12])))
+        need("v", ("put", 0))
+        for run in high:
+            D["old"] = v(V.tensor_copy(slots(T.old, run[0], len(run)), T.tb0[:].indirect(listed(run[0], len(run)))))
 
-    def newest():
+    def newest(a):
         need("v", ("put", 0), ("put", 1))
-        D["last"] = tt(T.pl[:, 384:640], T.tb0[:], T.tb1[:], A.max)
+        D["last"] = tt(T.tl[:, a:a + 128], T.tb0[:, a:a + 128], T.tb1[:, a:a + 128], A.max)
+
+    lo, hi = W4 * where[0][0], W4 * where[4][0]
+    part = {"lo": ([(T.pl, lo, ("look", 0))], W4, 8, 0, 0, 0, p1, lo // 8), "hi": ([(T.old, lo, "earlier")], W4, 8, 0, W4, 0, p1, hi // 8),
+            "end": ([(T.tl, 0, "last")], 256, 4, 8, 2 * W4, 192, pc, 48)}
 
     def merge():
-        need("v", "old", ("look", 1 - low))
-        D["earlier"] = tt(T.pl[:, W4 * (1 - low):W4 * (2 - low)], T.lk[:, W4 * (1 - low):W4 * (2 - low)], T.old[:], A.max)
+        need("v", "old", ("look", 1))
+        D["earlier"] = tt(T.old[:, lo:lo + W4], T.pl[:, hi:hi + W4], T.old[:, hi:hi + W4], A.max)
 
-    def select(a, b, n, m, ready):
-        need("s", ready, v_mk)
-        for k in range(n):
-            D["sel", a] = s(S.activation(T.dg[:, a + k:b:n], T.pl[:, a + k:b:n], F.Identity, scale=T.mk[:, m + k:m + k + 1]))
+    def select(name, q):
+        srcs, w, n, m, a = part[name][:5]
+        for i, (buf, c, ready) in enumerate(srcs):
+            need(q, ready)
+            for k in range(n):
+                o, x, z = T.dg[:, a + n * i + k:a + w * len(srcs):n * len(srcs)], buf[:, c + k:c + w:n], T.mk[:, m + k:m + k + 1]
+                D["sel", name] = s(S.activation(o, x, F.Identity, scale=z)) if q == "s" else ts(o, x, z, None, A.mult)
 
-    def gather_up(a, b):
-        need("v", ("sel", a))
-        D["up", a] = v(V.tensor_tensor_scan(T.dd[:, a:b], T.keep[:, a:b], T.dg[:, a:b], 0.0, A.mult, A.add))
+    def gather_up(name):
+        srcs, w, n, m, a, k = part[name][:6]
+        need("v", ("sel", name))
+        D["up", name] = v(V.tensor_tensor_scan(T.dd[:, a:a + w * len(srcs)], T.keep[:, k:k + w * len(srcs)], T.dg[:, a:a + w * len(srcs)], 0.0, A.mult, A.max))
 
-    def address(a, b, n, c, o):
-        need("v", ("up", a))
-        D["op", a] = ts(T.op[:, o:o + (b - a) // n], T.dd[:, a + n - 1:b:n], c, None, A.add)
+    def address(name):
+        srcs, w, n, m, a, k, c, o = part[name]
+        need("v", ("up", name))
+        D["op", name] = ts(T.op[:, o:o + w // n], T.dd[:, a + n * len(srcs) - 1:a + w * len(srcs):n * len(srcs)], c, None, A.add)
 
     def expert(h, ready):
         a, banks, hh = (336, 144)[h], [4 * h + i for i in range(4)], T["hh%d" % h]
@@ -363,34 +415,32 @@ def rank_program(g, core, T, topo):
             s_r = s(S.activation(hh[:, i:4 * W4:4], T["ps%d" % banks[i]][:, 0:W4], F.Relu, scale=0.05))
             need("v", tm[i + 1])
             v_r = ts(hh[:, i + 1:4 * W4:4], T["ps%d" % banks[i + 1]][:, 0:W4], 0.0, 0.05, A.max, A.mult)
+        if links:
+            links.pop(0)()
+            behind.extend(rest[:1])
+            del rest[:1]
         need("v", s_r, v_r)
         x = v(V.quantize_mx(T.mq[:, a:a + W4], T.mc[:, a:a + W4], hh[:, 0:4 * W4]))
-        back = [[(d, "m", 336 + CK * k, "m", 528 + in_far(d), "rf%d" % far_of(d).index(rank)) for k, d in enumerate(far)],
-                [(d, "m", W4 + CK * k, "m", in_near(d), "rn") for k, d in enumerate(others)]]
-        if not (HOLD[rank] and h):
-            need("p", x)
-            send(back[h] + (back[1] if HOLD[rank] else []))
+        need("p", x)
+        for z in "qc":
+            if h == 0:
+                send(z, [(d, "m", 336 + CK * k, "m", 528 + in_far(d), "r%d" % rank, far_m[z][k]) for k, d in enumerate(far)])
+            else:
+                send(z, [(d, "m", W4 + CK * k, "m", CK * (2 - near_of(d).index(rank)), "r%d" % rank, near_m[z][k]) for k, d in enumerate(others)])
         return [s_r, v_r, x]
 
     free = [None, None]
-    arrived = [[AF], [AN, ("tile", 1), ("read", 1), ("srk", 1)]]
-    place = sorted(X[1]).index(rank)
-    shifted(1)
-    weights(0), weights(1)
-    links, rest = chain(1), [do(weights, 2), do(weights, 3)] + [do(unit, b) for b in range(4)]
-    for step in STEPS[place]:
+    arrived = [[AF], [AN, ("tile", where[rank][0]), ("read", 1), ("srk", 1)]]
+    for step in STEPS[rank]:
         if step in ("f", "n"):
+            behind = []
             free["fn".index(step)] = expert("fn".index(step), arrived["fn".index(step)])
-        elif step == "m":
-            older(), newest(), merge()
-        elif step == "s":
-            select(0, 384, 8, 0, "earlier")
-            select(384, 640, 4, 8, "last")
-        elif step == "a":
-            gather_up(0, 384), gather_up(384, 640), address(0, 384, 8, p1, 0), address(384, 640, 4, pc, 48)
+            both(*behind)()
         else:
-            weave(links[:step], rest)
-            links = links[step:]
+            weave([links.pop(0) for k in range(min(step, len(links)))], rest)
+    select("lo", "s")
+    gather_up("lo"), older(), newest(0), merge(), address("lo"), newest(128)
+    late = [do(gather_up, "hi"), do(address, "hi")]
 
     banks = [free[0] + free[1], free[0] + free[1]]
     turns = [0]
@@ -398,12 +448,12 @@ def rank_program(g, core, T, topo):
     def unpack(a, n, arrived):
         k = turns[0] % 2
         turns[0] += 1
-        need("t", "eb", arrived, *banks[k])
+        need("t", "eb", *(arrived + banks[k]))
         return k, [t(PE.matmul_mx(T["ps%d" % (4 * k + b)][:, 0:n], T.eq[:, 128 * b:128 * b + 128], T.ec[:, 128 * b:128 * b + 128],
                                   T.mq[:, a:a + n], T.mc[:, a:a + n], True, True)) for b in range(4)]
 
     def fetch(q, u, b, e, c, n, *ready):
-        h, a = where[e]
+        h, a = lies[e]
         buf, at = (T.pb, HALF * (b // 2) + 8) if e == 0 else (T["ds%d" % h], 4 * W2 * (b // 2) + W2 * a)
         o, i = buf[:, at + b % 2:at + W2 * n:2], T["ps%d" % (4 * u[0] + b)][:, c:c + CK * n]
         need(q, u[1][b], *ready)
@@ -414,42 +464,51 @@ def rank_program(g, core, T, topo):
     def add(upto):
         for e in range(added[0] + 1, upto + 1):
             h, a = where[e]
-            need("v", ("op", 0), *(ready.get(e, []) + ready[0]))
             o, k = 8 + W2 * e, 24 * h + 6 * a
             for c in range(2):
-                need("v", *([("add", c)] if e > 1 else []))
-                d = 4 * W2 * c + W2 * a
+                need("v", ("op", "hi" if e >= 4 else "lo"), *(ready.get(e, [])[:2 * c + 2] + ([("add", c)] if e > 1 else ready[0][:2 * c + 2])))
+                d = 4 * W2 * c + W2 * lies[e][1]
                 D["add", c] = tt(T.pb[:, HALF * c + o:HALF * c + o + W2], T.pb[:, HALF * c:HALF * c + o].indirect(T.op[:, k:k + 6]),
-                                 T["ds%d" % h][:, d:d + W2], A.add)
+                                 T["ds%d" % lies[e][0]][:, d:d + W2], A.add)
             added[0] = e
+            if late:
+                late.pop(0)()
 
-    def far_in(k, queues):
-        u = unpack(528 + CK * (k + 1) - 128, 128, RF[k])
-        banks[u[0]] = ready[far[k]] = [fetch(queues[b % 2], u, b, far[k], 128 - CK, 1) for b in range(4)][-2:]
-
-    if 0 in far:
-        for k in range(3):
-            far_in(k, "ss")
-        u = unpack(0, W4, RN)
-        banks[u[0]] = ready[4] = [fetch("s", u, b, X[1][0], 0, 4) for b in range(4)][-1:]
-        add(2)
-    else:
-        u = unpack(0, W4, RN)
-        one = [fetch("sv"[b % 2], u, b, e, CK * where[e][1], 1) for b in range(4) for e in (0, 1)]
-        ready[0] = one[-3:]
-        pair = min((2, 3), key=lambda e: where[e][1])
-        banks[u[0]] = ready[2] = [fetch("s", u, b, pair, CK * where[pair][1], 2, *one[-1:] * (b % 2)) for b in (0, 2, 1, 3)][-1:]
-        for k in range(3):
-            far_in(k, "ss")
-        add(6)
-    far_in(3, "sv")
+    for group, shared in UNITS[side(rank)]:
+        if group[0] == END[side(rank)]:
+            select("hi", "s")
+        at = sorted(lies[e][1] for e in group)
+        n = max(128, CK * (at[-1] + 1 - at[0]))
+        if group[0] in far:
+            a = 528 + CK * (at[-1] + 1) - n
+            u = unpack(a, n, [RB[e] for e in far[:at[-1] + 1]])
+        else:
+            a = CK * at[0]
+            u = unpack(a, n, [RB[e] for e in back[at[0]:3]])
+        col = lambda e: CK * lies[e][1] + 528 * (e in far) - a
+        lead = group[:1 + (group[0] == 0)] if shared else []
+        if lead:
+            final = group == UNITS[side(rank)][-1][0]
+            add(group[0] - 1)
+            if final:
+                gather_up("end")
+            x = [fetch("sv"[b % 2], u, b, e, col(e), 1) for b in range(4) for e in lead]
+            ready.update({e: x[k::len(lead)] for k, e in enumerate(lead)})
+            banks[u[0]] = x[-2 * len(lead):]
+            if final:
+                address("end")
+        for run in runs(sorted((e for e in group if e not in lead), key=col), lambda e, f: e and f and col(f) == col(e) + CK):
+            banks[u[0]] = [fetch("s", u, b, run[0], col(run[0]), len(run), *x[-1:] * (b % 2) if lead else []) for b in range(4)]
+            ready.update({e: banks[u[0]] for e in run})
+        if group[0] == END[side(rank)]:
+            select("end", "s")
     add(7)
-    need("v", ("add", 1), ("op", 384))
-    need("s", ("add", 1), ("op", 384))
+    need("v", ("add", 1), ("op", "end"))
+    need("s", ("add", 1), ("op", "end"))
     for a in (0, 512):
         part = lambda c: (T.yt[:, c:c + 256], T.pb[:].indirect(T.op[:, 48 + c // 16:64 + c // 16]))
         need("y", v(V.tensor_copy(*part(a))), s(S.activation(*part(a + 256), F.Copy)))
         g.sync.dma_start(T.y[:, a:a + 512], T.yt[:, a:a + 512]).then_inc(T.sem.dy, 16)
 
-    need("p", ("ls", ls[0]), DWG, DX, DW, AF, AN, *RF, RN, ("dy", 32))
+    need("p", ("ls", ls[0]), DWG, DX, DW, AF, AN, *RB.values(), ("dy", 32))
     need("p", *[(q, cnt[q]) for q in ("v", "s", "t", "p")])

from concourse.bass import DstId, RemoteDMATransfer
from concourse.mybir import dt, AluOpType as A, ActivationFunctionType as F

CK = 48
W4 = 4 * CK
SB = [[5, 6, 7], [4, 5, 6, 7]]
SW = 257
W2 = 2 * CK
HALF = 8 + 8 * W2

FIRST = [[4, 5, 6, 7], [0, 1, 2, 3]]
EVEN, ODD, LOW, HIGH = [0, 2, 4, 6], [1, 3, 5, 7], [8, 9, 10, 11], [12, 13, 14, 15]
PAIRS = [[0, 1], [2, 3], [4, 5], [6, 7]]
CALLS = [[[("q", [4, 7], [EVEN, LOW]), ("c", [4, 5, 6, 7], [ODD[:2], ODD[2:3], ODD[3:], LOW]), ("q", [5], [EVEN]), ("q", [6], [EVEN])],
          [("q", [0, 1, 2, 3], [LOW, HIGH, ODD]), ("c", [0, 1, 2, 3], [LOW, HIGH, EVEN])]],
         [[("q", [0], [EVEN]), ("c", [0, 1, 2, 3], [[k] for k in ODD]), ("q", [1], [EVEN]), ("q", [2], [EVEN])],
          [("q", [3, 4, 5, 6, 7], [EVEN, LOW, HIGH, ODD]), ("c", [4, 5, 6, 7], [LOW, HIGH, EVEN])]]]
ROUND = 7
AT = [[0, 3, 6, 9], [0, 3, 6, 9]]
UNITS = [[([0, 1, 2, 3], True), ([4], False), ([5], False), ([6], False), ([7], True)],
         [([0], False), ([1], False), ([2], False), ([4, 5, 6, 7], False), ([3], True)]]
END = [0, 2]
STEPS = [(2, "f", 2, "n", 1), (3, "f", 1, "n", 1), (4, "f", "n", 1), (5, "n", "f")] * 2

ENG = {"rf": {z: PAIRS for z in "qc"},
       "rn": {"q": [LOW, HIGH[:2], HIGH[2:]], "c": [HIGH, LOW[:2], LOW[2:]]}}

SCRATCH = {}


def _sbuf(dtype, names):
    for w in names.split():
        n, c = w.split(":")
        for m in ([n[:-1] + "0", n[:-1] + "1"] if n.endswith("@") else [n]):
            SCRATCH[m] = ("sbuf", [128, int(c)], dtype)


_sbuf("bfloat16", "wgs:32 xs:1024 xp:1024 w1s:2048 ones:128 z:516 col:256 blk:256 tok0:128 tokv:128 hh@:768 gt@:512 cmp@:2048 cs@:1024 sg@:%d "
      "eqb@:256 es@:256 wn@:256 dp@:96 tw@:96 yl@:14 xg@:768" % (8 * SW))
for _d, _s in (("float8_e4m3fn_x4", "q"), ("uint8", "c")):
    _sbuf(_d, " ".join("%s%s%s" % (w[0], _s, w[1:]) for w in "x:256 w:512 e:512 t:192 n:528 m:720 g@:128".split()))
_sbuf("int32", "ic:1 pi:8")
_sbuf("float32", "e4:64 pf:9 do0:6 mk:12 idr:384 pl:384 old:384 tb@:256 tl:256 dg:640 keep:448 dd:640")
_sbuf("float32", "ds@:768 pb:%d yt:1024 tt@:256 ac@:24" % (2 * HALF))
_sbuf("uint16", "go:64 do:6 op:112 ru@:8 ol@:14 of@:14")
for _b in range(8):
    SCRATCH["ps%d" % _b] = ("psum", [128, 512], "float32")

SEMAPHORES = ["v", "t", "s", "p", "dwg", "dx", "dw", "af", "an", "ls", "dy"] + ["r%d" % e for e in range(8)]


def runs(items, follows):
    out = []
    for e in items:
        if out and follows(out[-1][-1], e):
            out[-1].append(e)
        else:
            out.append([e])
    return out


def rank_program(g, core, T, topo):
    rank = T.rank_of(core)
    N = len(T.cores)
    near_of = lambda r: [k for k in range(N) if k != r and topo.chip(T.cores[k]) == topo.chip(T.cores[r])]
    far_of = lambda r: [k for k in range(N) if topo.chip(T.cores[k]) != topo.chip(T.cores[r])]
    helper = {r: [c for c in topo.cores_of(T.cores[r]) if topo.die(c) != topo.die(T.cores[r])][k] for k, r in enumerate(far_of(ROUND))}

    def transfer(z, to, src, a, dst, b, sem, eng):
        rid, pid, _ = topo.addr(to)
        sa, da = T[src + z][:, a:a + CK], T[dst + z][:, b:b + CK]
        if z == "q":
            sa, da = sa.bitcast(dt.uint8), da.bitcast(dt.uint8)
        return RemoteDMATransfer(dst_ids=[DstId(rid=rid, pnc=pid)], dma_engine_mask=sum(1 << e for e in eng), remote_sem=T.sem[sem], src=sa, dst=da)

    if rank is None:
        for k, r in enumerate(far_of(ROUND)):
            if helper[r] == core:
                eng = topo.engines(core, T.cores[ROUND])
                g.wait_ge(T.sem.af, 2 * len(LOW))
                for z, places in (("q", EVEN), ("c", EVEN)):
                    g.remote_dma_fused([transfer(z, T.cores[ROUND], "t", 0, "n", 336 + CK * k, "af", [eng[i] for i in places])], local_sem=T.sem.ls)
                g.wait_ge(T.sem.ls, 2 * len(EVEN))
        return
    others, far = near_of(rank), far_of(rank)
    side = lambda r: int(0 in far_of(r))
    X = [sorted((e for e in range(N) if (e in FIRST[side(rank)]) != h), key=lambda e: (e == rank, e)) for h in range(2)]
    where = {e: (h, a) for h in range(2) for a, e in enumerate(X[h])}
    back = others[::-1] + [rank]
    lies = {e: (c, a) for c, es in enumerate((far, back)) for a, e in enumerate(es)}
    far_e = topo.engines(core, T.cores[far[0]])
    near_e = [e for e in topo.engines(core, T.cores[others[0]]) if e not in far_e]

    Q = {"v": g.vector, "t": g.tensor, "s": g.scalar, "p": g, "y": g.sync}
    cnt = {"v": 0, "t": 0, "s": 0, "p": 0}
    seen = {}
    D = {}

    def need(q, *toks):
        for s, n in [D[k] if k in D else k for k in toks]:
            if seen.get((q, s), 0) < n:
                Q[q].wait_ge(T.sem[s], n)
                seen[(q, s)] = n

    def done(q, ins):
        ins.then_inc(T.sem[q], 1)
        cnt[q] += 1
        return (q, cnt[q])

    def weave(steps, fill):
        for step in steps:
            step()
            if fill:
                fill.pop(0)()

    V, S, PE = g.vector, g.scalar, g.tensor
    v = lambda ins: done("v", ins)
    s = lambda ins: done("s", ins)
    t = lambda ins: done("t", ins)
    p = lambda ins: done("p", ins)
    ts = lambda out, in0, s1, s2, *ops: v(V.tensor_scalar(out, in0, s1, s2, *ops))
    tt = lambda out, a, b, op: v(V.tensor_tensor(out, a, b, op))
    both = lambda *fs: lambda: [f() for f in fs]

    g.scalar.dma_start(T.wgs[:], T.wg[:, 0:32]).then_inc(T.sem.dwg, 16)
    g.sync.dma_start(T.xs[:], T.x[:]).then_inc(T.sem.dx, 16)
    g.sync.dma_start(T.w1s[:], T.w1[:]).then_inc(T.sem.dw, 16)
    DWG, DX, DW = ("dwg", 16), ("dx", 16), ("dw", 16)

    imp = dict(allow_small_or_imprecise_dtypes=True)
    p_ic = p(g.iota(T.ic[:], [[0, 1]], 0, 1))
    v(V.memset(T.ones[:], 1.0))
    need("p", v(V.memset(T.z[:], 0.0)))
    p_z = p(g.affine_select(T.z[:, 3:515:4], T.ones[:], [[-1, 128]], A.is_equal, 0.0, 0, 1))
    p_e4 = p(g.iota(T.e4[:], [[4, N], [0, 8]], 0, 0, **imp))
    p_do = p(g.iota(T.do0[:], [[16, 3], [0, 2]], 0, 0, **imp))
    p_col = p(g.iota(T.col[:], [[0, 8], [1, 32]], 0, 0, **imp))
    p_tok = p(g.iota(T.tok0[:], [[32, 8], [1, 16]], 0, 0, **imp))
    for h in range(2):
        p_m = p(g.iota(T["sg%d" % h][:, SW - 1:8 * SW:SW], [[-32, 8]], -32, 0, **imp))
    fill = lambda ap, n, c=0: p(g.iota(ap, [[0, n]], c, 0, **imp))
    p_wn = [fill(T["wn%d" % h][:, 0:CK], CK) for h in range(2)]
    need("p", fill(T.keep[:], 448, 1))
    fill(T.keep[:, 0:192:8], 24)
    fill(T.keep[:, 192:448:4], 64)
    for h in range(2):
        fill(T["tb%d" % h][:], 256)
    p_id = p(g.iota(T.idr[:], [[W2, N], [2, CK]], 8, 0, **imp))

    def unit(b):
        need("v", p_z)
        D["eb"] = v(V.quantize_mx(T.eq[:, 128 * b:128 * b + 128], T.ec[:, 128 * b:128 * b + 128], T.z[:, 3 - b:515 - b]))

    need("v", p_ic)
    for k, m in enumerate((3, 31, 16, 15, 12, 14, 1, 2)):
        x = ts(T.pi[:, k:k + 1], T.ic[:], m, None, A.bitwise_and)
    unit(0)
    need("v", x)
    v_pf = v(V.tensor_copy(T.pf[:, 0:8], T.pi[:]))
    unit(1)
    p3, p31, p16, p15, p12, p14, p1, p2, pc = [T.pf[:, k:k + 1] for k in range(9)]
    need("v", v_pf, p_e4, p_do)
    order = sorted(X[0]) + sorted(X[1])
    for run in runs(order, lambda e, f: f == e + 1):
        k = order.index(run[0])
        v_go = ts(T.go[:, 8 * k:8 * (k + len(run))], T.e4[:, 8 * run[0]:8 * (run[0] + len(run))], p3, None, A.add)
    v_do = ts(T.do[:], T.do0[:], p15, None, A.add)
    unit(2), unit(3)
    zero = lambda ap: lambda: v(V.memset(ap, 0.0))
    slots = lambda buf, e, n=1: buf[:, W4 * where[e][0] + CK * where[e][1]:W4 * where[e][0] + CK * (where[e][1] + n)]
    small = [zero(slots(T.pl, 0)), zero(slots(T.pl, 4)), zero(T.pb[:, 0:8]), zero(T.pb[:, HALF:HALF + 8]),
             lambda: ts(pc, p2, HALF / 2, p1, A.mult, A.add), lambda: ts(T.mk[:, 0:8], T.col[:, 0:16:2], p14, None, A.is_equal),
             lambda: ts(T.mk[:, 8:12], T.col[:, 0:16:4], p12, None, A.is_equal)]
    need("v", DWG, v_go)
    gate = lambda h, a, b: (T["gt%d" % h][:, 16 * a:16 * b], T.wgs[:, 0:32].indirect(T.go[:, 32 * h + a:32 * h + b]))
    v_gt0 = v(V.tensor_copy(*gate(0, 0, 16)))
    need("s", DWG, v_go)
    s_gt0 = s(S.activation(*gate(0, 16, 32), F.Copy))
    s_gt1 = s(S.activation(*gate(1, 8, 32), F.Copy))
    v_gt = v(V.tensor_copy(*gate(1, 0, 8)))
    need("v", s_gt0, v_gt0)
    v_gq = [v(V.quantize_mx(T.gq0[:, 0:128], T.gc0[:, 0:128], T.gt0[:, 0:512])), None]

    need("v", DX)
    v_xq = v(V.quantize_mx(T.xq[:, 0:256], T.xc[:, 0:256], T.xs[:, 0:1024]))
    plane = lambda k: (T.xp[:, 256 * k:256 * k + 256], T.xs[:, k:1024:4])
    sv, ss = [T.ps4, T.ps6], [T.ps5, T.ps7]

    def score(h):
        need("t", v_xq, v_gq[h])
        for n, bank in (("sv", sv), ("ss", ss)):
            D[n, h] = t(PE.matmul_mx(bank[h][:, 0:256], T["gq%d" % h][:, 0:128], T["gc%d" % h][:, 0:128], T.xq[:, 0:256], T.xc[:, 0:256], True, True))

    slot = lambda h, b: T["cs%d" % h][:, 128 * b + 127:128 * b + 128]

    def own(h, a, b):
        need("v", ("sv", h))
        x = v(V.transpose(T["tt%d" % h][:, 32 * a:32 * b], sv[h][:, 32 * a:32 * b]))
        D.update({("own", h, k): x for k in range(a, b)})

    def equal(h):
        need("v", *[("own", h, k) for k in range(8)])
        D["eq", h] = tt(T["eqb%d" % h][:], sv[h][:, 0:256], T["tt%d" % h][:], A.is_equal)

    def later(h):
        need("v", ("eq", h), v_blk)
        D["es", h] = v(V.tensor_tensor_scan(T["es%d" % h][:], T.blk[:], T["eqb%d" % h][:], 0.0, A.mult, A.subtract))

    def compare(h, b, parts="ab"):
        P, cm, m, o = sv[h], T["cmp%d" % h], 32 * (b + 1), T["tt%d" % h][:, 32 * b:32 * b + 1]
        need("v", ("own", h, b))
        if "a" in parts:
            ts(cm[:, 256 * b:256 * b + m], P[:, 0:m], o, None, A.is_ge)
        if "b" in parts:
            D["read", h] = D["cmp", h, b] = ts(cm[:, 256 * b + m:256 * b + 256], P[:, m:256], o, None, A.is_gt)

    def total(h, *blocks):
        cm = T["cmp%d" % h]
        for b in blocks:
            need("v", ("cmp", h, b), ("es", h))
            D["vrk", h] = v(V.tensor_tensor_scan(T["cs%d" % h][:, 128 * b:128 * b + 128], cm[:, 256 * b:256 * b + 128], cm[:, 256 * b + 128:256 * b + 256],
                                                 T["es%d" % h][:, 32 * b + 31:32 * b + 32], A.add, A.add))

    def signs(h):
        for b in SB[h]:
            need("s", ("ss", h), ("own", h, b))
            D["sign", h, b] = s(S.activation(T["sg%d" % h][:, SW * b:SW * b + 256], ss[h][:, 0:256], F.Sign, bias=T["tt%d" % h][:, 32 * b:32 * b + 1], scale=-1.0))

    def sums(h, blocks):
        sg, ac = T["sg%d" % h], T["ac%d" % h]
        for b in blocks:
            need("s", ("sign", h, b), p_m)
            m = SW * b + 32 * (b + 1)
            lo, hi = sg[:, SW * b:m], sg[:, m:SW * b + SW]
            D["part", h, b] = s(S.activation(lo, lo, F.Relu, accum_out=ac[:, b:b + 1]))
            if b < 7:
                D["part", h, b] = s(S.activation(hi, hi, F.Relu, scale=-1.0, accum_out=ac[:, 8 + b:9 + b]))
            for k in range(max(b - 1, SB[h][0]), b + (b == 7)):
                need("s", ("part", h, k))
                D["sum", h, k] = s(S.activation(ac[:, 16 + k:17 + k], ac[:, k:k + 1], F.Identity, scale=-1.0, bias=ac[:, 8 + k:9 + k] if k < 7 else 256.0))

    def settle(h):
        for b in SB[h]:
            need("s", ("sum", h, b), ("es", h))
            D["srk", h] = s(S.activation(slot(h, b), T["ac%d" % h][:, 16 + b:17 + b], F.Identity, bias=T["es%d" % h][:, 32 * b + 31:32 * b + 32]))

    ls = [0]
    pick_e = lambda sets: [[(far_e + near_e)[k] for k in ks] for ks in sets]
    near_m, far_m = [{z: pick_e(ENG[n][z]) for z in "qc"} for n in ("rn", "rf")]
    out = [{(z, d): eng for z, ds, sets in CALLS[side(r)][0] + CALLS[side(r)][1] for d, eng in zip([d for d in ds if d != r], pick_e(sets))}
           for r in range(N)]
    AF, AN = [(n, sum(len(out[r][z, rank]) for r in rs for z in "qc")) for n, rs in (("af", far), ("an", others))]
    RB = {e: ("r%d" % e, sum(len(far_m[z][far_of(e).index(rank)] if e in far else near_m[z][near_of(e).index(rank)]) for z in "qc")) for e in far + others}

    def send(z, parts):
        tr = []
        for d, src, a, dst, b, sem, eng in parts:
            if (d, sem) == (ROUND, "af"):
                tr.append(transfer(z, helper[rank], src, a, "t", 0, sem, eng))
            else:
                tr.append(transfer(z, T.cores[d], src, a, dst, b, sem, eng))
            ls[0] += len(eng)
        g.remote_dma_fused(tr, local_sem=T.sem.ls)

    in_far = lambda d: CK * far_of(d).index(rank)
    in_near = lambda d: CK * near_of(d).index(rank)

    def dispatch(h):
        B = lambda n: T["%s%d" % (n, h)]
        x = [None]

        def offsets():
            need("v", ("vrk", h), ("srk", h))
            x[0] = v(V.tensor_copy(B("ru")[:], B("cs")[:, 127:1024:128]))

        def scatter():
            need("v", x[0], v_tok, p_wn[h])
            x[0] = v(V.tensor_copy(B("wn")[:, 0:256].indirect(B("ru")[:, 0:8]), T.tokv[:, 0:128]))

        def twice():
            need("v", x[0], v_do)
            x[0] = v(V.tensor_copy(B("dp")[:], B("wn")[:, 0:CK].indirect(T.do[:, 0:6])))

        def turn():
            need("v", x[0])
            x[0] = v(V.transpose(B("tw")[:], B("dp")[:]))

        def collect(a, b):
            need("v", x[0])
            for e in X[h][a:b]:
                k, c = AT[h][where[e][1]], 32 * sorted(X[h]).index(e)
                D["yl", h, a] = tt(B("yl")[0:32, k:k + 3], B("tw")[c:c + 32, 0:96:32], B("tw")[c:c + 32, 16:96:32], A.add)

        def spread(a, b):
            need("v", ("yl", h, a))
            k = AT[h][a]
            for c in range(0, 128, 32):
                D["of", h] = D["of", h, a] = v(V.tensor_copy(B("of")[c:c + 32, k:k + 3 * (b - a)], B("yl")[0:32, k:k + 3 * (b - a)]))

        def pick(q, a, b):
            need(q, s_xp, v_xp, ("of", h, a), *([("tile", h)] if a else []))
            for k in (0, 1) if q == "s" else (2, 3):
                o, i = B("xg")[:, 4 * CK * a + k:4 * CK * b:4], T.xp[:, 256 * k:256 * k + 256].indirect(B("of")[:, AT[h][a]:AT[h][a] + 3 * (b - a)])
                D["xg", q] = s(S.activation(o, i, F.Copy)) if q == "s" else v(V.tensor_copy(o, i))

        def pack(a, b):
            need("v", ("xg", "v"), ("xg", "s"))
            src, n = ["n" if rank in es else "t" for es in X], max(128, CK * b)
            D["tile", h] = v(V.quantize_mx(T[src[h] + "q"][:, CK * a:n], T[src[h] + "c"][:, CK * a:n], B("xg")[:, 4 * CK * a:4 * n]))
            need("p", ("tile", h))
            calls = CALLS[side(rank)][h]
            for z, ds, _ in calls[:1] if b < 4 else calls[a:]:
                send(z, [(d, src[where[d][0]], CK * where[d][1], "n", 336 + in_far(d) if d in far else W4 + in_near(d), "af" if d in far else "an", out[rank][z, d])
                         for d in ds if d != rank])

        return [offsets, scatter, twice, turn], collect, spread, pick, pack

    def weights(i):
        need("v", DW)
        D["wq"] = v(V.quantize_mx(T.wq[:, 128 * i:128 * i + 128], T.wc[:, 128 * i:128 * i + 128], T.w1s[:, 512 * i:512 * i + 512]))

    def shifted(h):
        need("v", ("of", h))
        D["ol", h] = v(V.tensor_copy(T["ol%d" % h][:, AT[h][1] + 1:AT[h][3] + 4], T["of%d" % h][:, AT[h][1]:AT[h][3] + 3]))

    def listed(e, n=1):
        h, k = where[e][0], AT[where[e][0]][where[e][1]]
        return T["ol%d" % h][:, k + 1:k + 1 + 3 * n] if k % 2 else T["of%d" % h][:, k:k + 3 * n]

    def chain(c):
        steps = []
        for e in range(4 * c, 4 * c + 4):
            def look(e=e):
                need("v", ("put", c), ("ol", where[e][0]))
                D["look", c] = v(V.tensor_copy(slots(T.pl, e), T["tb%d" % c][:].indirect(listed(e))))

            def put(e=e):
                need("v", p_id, ("ol", where[e][0]), *([("look", c)] if e % 4 else []))
                D["put", c] = v(V.tensor_copy(T["tb%d" % c][:].indirect(listed(e)), T.idr[:, CK * e:CK * e + CK]))
            steps += [look, put] if e % 4 else [put]
        return steps

    score(0)
    for k in (2, 3):
        v_xp = v(V.tensor_copy(*plane(k)))
    need("v", p_col, p_tok)
    v_blk = ts(T.blk[:], T.col[:], p31, None, A.not_equal)
    need("v", s_gt1, v_gt)
    v_gq[1] = v(V.quantize_mx(T.gq1[:, 0:128], T.gc1[:, 0:128], T.gt1[:, 0:512]))
    score(1)
    v_tok = ts(T.tokv[:], T.tok0[:], p16, None, A.add)
    need("s", DX)
    for k in (0, 1):
        s_xp = s(S.activation(*plane(k), F.Copy))
    do = lambda f, *a: lambda: f(*a)
    own(0, 5, 8), own(0, 0, 1), own(0, 1, 5)
    signs(0), sums(0, SB[0])
    compare(0, 0), equal(0), compare(0, 1), later(0)
    settle(0)
    compare(0, 2), own(1, 4, 8)
    signs(1), sums(1, SB[1])
    compare(0, 3), compare(0, 4), own(1, 0, 4), total(0, 0, 1, 2, 3, 4), equal(1)
    steps = lambda lists, collect, spread, pick, pack: lists + [do(collect, 0, 4), both(do(spread, 0, 4), do(pick, "s", 0, 4)), do(pick, "v", 0, 4), do(pack, 0, 4)]
    weave(steps(*dispatch(0)), [both(do(compare, 1, 0, "a"), do(compare, 1, 1, "a")), both(do(later, 1), do(settle, 1)), do(compare, 1, 0, "b"), do(compare, 1, 1, "b"),
                                do(compare, 1, 2), do(compare, 1, 3, "a"), both(do(compare, 1, 3, "b"), do(total, 1, 0, 1, 2))])
    total(1, 3), shifted(0), small.pop()()
    weave(steps(*dispatch(1)), [both(*small[0:2]), do(weights, 0), both(*small[2:4]), do(weights, 1), do(weights, 2), both(*small[4:6]), do(weights, 3)])
    links, rest = chain(where[0][0]), chain(where[4][0])
    shifted(1)

    high = [run for h in range(2) for run in runs([e for e in X[h] if e >= 4], lambda e, f: AT[h][where[f][1]] == AT[h][where[e][1]] + 3)]

    def older():
        need("v", ("put", 0))
        for run in high:
            D["old"] = v(V.tensor_copy(slots(T.old, run[0], len(run)), T.tb0[:].indirect(listed(run[0], len(run)))))

    def newest(a):
        need("v", ("put", 0), ("put", 1))
        D["last"] = tt(T.tl[:, a:a + 128], T.tb0[:, a:a + 128], T.tb1[:, a:a + 128], A.max)

    lo, hi = W4 * where[0][0], W4 * where[4][0]
    part = {"lo": ([(T.pl, lo, ("look", 0))], W4, 8, 0, 0, 0, p1, lo // 8), "hi": ([(T.old, lo, "earlier")], W4, 8, 0, W4, 0, p1, hi // 8),
            "end": ([(T.tl, 0, "last")], 256, 4, 8, 2 * W4, 192, pc, 48)}

    def merge():
        need("v", "old", ("look", 1))
        D["earlier"] = tt(T.old[:, lo:lo + W4], T.pl[:, hi:hi + W4], T.old[:, hi:hi + W4], A.max)

    def select(name, q):
        srcs, w, n, m, a = part[name][:5]
        for i, (buf, c, ready) in enumerate(srcs):
            need(q, ready)
            for k in range(n):
                o, x, z = T.dg[:, a + n * i + k:a + w * len(srcs):n * len(srcs)], buf[:, c + k:c + w:n], T.mk[:, m + k:m + k + 1]
                D["sel", name] = s(S.activation(o, x, F.Identity, scale=z)) if q == "s" else ts(o, x, z, None, A.mult)

    def gather_up(name):
        srcs, w, n, m, a, k = part[name][:6]
        need("v", ("sel", name))
        D["up", name] = v(V.tensor_tensor_scan(T.dd[:, a:a + w * len(srcs)], T.keep[:, k:k + w * len(srcs)], T.dg[:, a:a + w * len(srcs)], 0.0, A.mult, A.max))

    def address(name):
        srcs, w, n, m, a, k, c, o = part[name]
        need("v", ("up", name))
        D["op", name] = ts(T.op[:, o:o + w // n], T.dd[:, a + n * len(srcs) - 1:a + w * len(srcs):n * len(srcs)], c, None, A.add)

    def expert(h, ready):
        a, banks, hh = (336, 144)[h], [4 * h + i for i in range(4)], T["hh%d" % h]
        need("t", "wq", *ready)
        tm = [t(PE.matmul_mx(T["ps%d" % k][:, 0:W4], T.wq[:, 128 * i:128 * i + 128], T.wc[:, 128 * i:128 * i + 128],
                             T.nq[:, a:a + W4], T["nc"][:, a:a + W4], True, True)) for i, k in enumerate(banks)]
        for i in (0, 2):
            need("s", tm[i])
            s_r = s(S.activation(hh[:, i:4 * W4:4], T["ps%d" % banks[i]][:, 0:W4], F.Relu, scale=0.05))
            need("v", tm[i + 1])
            v_r = ts(hh[:, i + 1:4 * W4:4], T["ps%d" % banks[i + 1]][:, 0:W4], 0.0, 0.05, A.max, A.mult)
        if links:
            links.pop(0)()
            behind.extend(rest[:1])
            del rest[:1]
        need("v", s_r, v_r)
        x = v(V.quantize_mx(T.mq[:, a:a + W4], T.mc[:, a:a + W4], hh[:, 0:4 * W4]))
        need("p", x)
        for z in "qc":
            if h == 0:
                send(z, [(d, "m", 336 + CK * k, "m", 528 + in_far(d), "r%d" % rank, far_m[z][k]) for k, d in enumerate(far)])
            else:
                send(z, [(d, "m", W4 + CK * k, "m", CK * (2 - near_of(d).index(rank)), "r%d" % rank, near_m[z][k]) for k, d in enumerate(others)])
        return [s_r, v_r, x]

    free = [None, None]
    arrived = [[AF], [AN, ("tile", where[rank][0]), ("read", 1), ("srk", 1)]]
    for step in STEPS[rank]:
        if step in ("f", "n"):
            behind = []
            free["fn".index(step)] = expert("fn".index(step), arrived["fn".index(step)])
            both(*behind)()
        else:
            weave([links.pop(0) for k in range(min(step, len(links)))], rest)
    select("lo", "s")
    gather_up("lo"), older(), newest(0), merge(), address("lo"), newest(128)
    late = [do(gather_up, "hi"), do(address, "hi")]

    banks = [free[0] + free[1], free[0] + free[1]]
    turns = [0]

    def unpack(a, n, arrived):
        k = turns[0] % 2
        turns[0] += 1
        need("t", "eb", *(arrived + banks[k]))
        return k, [t(PE.matmul_mx(T["ps%d" % (4 * k + b)][:, 0:n], T.eq[:, 128 * b:128 * b + 128], T.ec[:, 128 * b:128 * b + 128],
                                  T.mq[:, a:a + n], T.mc[:, a:a + n], True, True)) for b in range(4)]

    def fetch(q, u, b, e, c, n, *ready):
        h, a = lies[e]
        buf, at = (T.pb, HALF * (b // 2) + 8) if e == 0 else (T["ds%d" % h], 4 * W2 * (b // 2) + W2 * a)
        o, i = buf[:, at + b % 2:at + W2 * n:2], T["ps%d" % (4 * u[0] + b)][:, c:c + CK * n]
        need(q, u[1][b], *ready)
        return s(S.activation(o, i, F.Copy)) if q == "s" else v(V.tensor_copy(o, i))

    ready, added = {}, [0]

    def add(upto):
        for e in range(added[0] + 1, upto + 1):
            h, a = where[e]
            o, k = 8 + W2 * e, 24 * h + 6 * a
            for c in range(2):
                need("v", ("op", "hi" if e >= 4 else "lo"), *(ready.get(e, [])[:2 * c + 2] + ([("add", c)] if e > 1 else ready[0][:2 * c + 2])))
                d = 4 * W2 * c + W2 * lies[e][1]
                D["add", c] = tt(T.pb[:, HALF * c + o:HALF * c + o + W2], T.pb[:, HALF * c:HALF * c + o].indirect(T.op[:, k:k + 6]),
                                 T["ds%d" % lies[e][0]][:, d:d + W2], A.add)
            added[0] = e
            if late:
                late.pop(0)()

    for group, shared in UNITS[side(rank)]:
        if group[0] == END[side(rank)]:
            select("hi", "s")
        at = sorted(lies[e][1] for e in group)
        n = max(128, CK * (at[-1] + 1 - at[0]))
        if group[0] in far:
            a = 528 + CK * (at[-1] + 1) - n
            u = unpack(a, n, [RB[e] for e in far[:at[-1] + 1]])
        else:
            a = CK * at[0]
            u = unpack(a, n, [RB[e] for e in back[at[0]:3]])
        col = lambda e: CK * lies[e][1] + 528 * (e in far) - a
        lead = group[:1 + (group[0] == 0)] if shared else []
        if lead:
            final = group == UNITS[side(rank)][-1][0]
            add(group[0] - 1)
            if final:
                gather_up("end")
            x = [fetch("sv"[b % 2], u, b, e, col(e), 1) for b in range(4) for e in lead]
            ready.update({e: x[k::len(lead)] for k, e in enumerate(lead)})
            banks[u[0]] = x[-2 * len(lead):]
            if final:
                address("end")
        for run in runs(sorted((e for e in group if e not in lead), key=col), lambda e, f: e and f and col(f) == col(e) + CK):
            banks[u[0]] = [fetch("s", u, b, run[0], col(run[0]), len(run), *x[-1:] * (b % 2) if lead else []) for b in range(4)]
            ready.update({e: banks[u[0]] for e in run})
        if group[0] == END[side(rank)]:
            select("end", "s")
    add(7)
    need("v", ("add", 1), ("op", "end"))
    need("s", ("add", 1), ("op", "end"))
    for a in (0, 512):
        part = lambda c: (T.yt[:, c:c + 256], T.pb[:].indirect(T.op[:, 48 + c // 16:64 + c // 16]))
        need("y", v(V.tensor_copy(*part(a))), s(S.activation(*part(a + 256), F.Copy)))
        g.sync.dma_start(T.y[:, a:a + 512], T.yt[:, a:a + 512]).then_inc(T.sem.dy, 16)

    need("p", ("ls", ls[0]), DWG, DX, DW, AF, AN, *RB.values(), ("dy", 32))
    need("p", *[(q, cnt[q]) for q in ("v", "s", "t", "p")])
